import numpy as np, ml_dtypes
CORES = [40,64,80,88,96,104,120,144]
N = 8
BF = ml_dtypes.bfloat16
def gentries(a):
    return np.ascontiguousarray(a.reshape(8, 16, -1).transpose(0, 2, 1)).reshape(8, -1)
def gtable(e):
    e = np.asarray(e); return np.ascontiguousarray(e.reshape(8, -1, 16).transpose(0, 2, 1)).reshape(128, -1).astype(np.int32)
P, LG, I, K, M, RO = 4096, 12, 128, 48, 32, 4
RHO, KA, KB, LIGHT, HALF = 68, 17, 5, 48, 7168
def lists(rng):
    return np.argsort(rng.random((N, 8, 4, P)), axis=-1)
def parts(rng):
    x = rng.integers(0, 256, (N, 8, 16, P)); z = rng.integers(0, 256, (N, 8, 16, 4 * I))
    lev = rng.permuted(np.tile(np.array([0.95, 0.83, 0.74, 0.69, 0.65, 0.6, 0.53, 0.42]), (N, 1)), axis=1)
    w = np.minimum(rng.geometric(lev[:, :, None], (N, 8, P)), 8)
    return x, w, z, lists(rng)
def pack(x, w, z, mem):
    return {"pt": np.ascontiguousarray(x.reshape(N, 128, P)).astype(np.float32).astype(BF), "w0": np.ascontiguousarray(w).astype(np.float32).astype(BF),
            "z0": np.ascontiguousarray(z.reshape(N, 128, 4 * I)).astype(np.float32).astype(BF), "lm": np.stack([gtable(a.reshape(8, -1)) for a in mem])}
def total(rng, s):
    e = (s - P) >> 4; w = np.ones(P, np.int64); w[:e] = 8; w[e:e + s - P - 7 * e] = 2
    return rng.permutation(w)
def setup_inputs(rng):
    return pack(*parts(rng))
def setup_inputs_spread(rng):
    def uneven(n):
        v = np.floor(np.exp2(8 * rng.random((N, 8, 1, n))) * rng.random((N, 8, 16, n))).astype(np.int64)
        return np.where(rng.random(v.shape) < 0.5, v, 255 - v)
    x, z = uneven(P), uneven(4 * I)
    ex = rng.permuted(np.tile(np.array([1.0, 2.0, 3.0, 5.0, 8.0, 12.0, 16.0, 24.0]), (N, 1)), axis=1)
    w = 1 + np.minimum(np.floor(8 * rng.random((N, 8, P)) ** ex[:, :, None]).astype(np.int64), 7)
    return pack(x, w, z, lists(rng))
def setup_inputs_ends(rng):
    def two(n):
        e = 255 * rng.integers(0, 2, (N, 8, 16, n)); m = rng.integers(0, 7, (N, 8, 1, n))
        return np.where(m == 0, 0, np.where(m == 1, 255, e))
    x, z = two(P), two(4 * I); w = np.ones((N, 8, P), np.int64)
    s = rng.permuted(np.tile(np.array([0.02, 0.06, 0.1, 0.15, 0.3, 0.5]), (N, 1)), axis=1)
    w[:, 1:7] = np.where(rng.random((N, 6, P)) < s[:, :, None], 8, 1); w[:, 1:7, 0] = 8; w[:, 1:7, P - 1] = 8
    w[0::2, 0] = 8; w[1::2, 7] = 8
    z[:, 1:6:2, :, I - 1::I] = 255; z[:, 0:7:2, :, I - 1::I] = 0
    for r in (0, N - 1): x[r, 7] = 255 * (rng.random((16, P)) < 0.03125)
    z[0, 7] = 255; z[1, 7] = 255
    inner = np.arange(4 * I) % I < I - 1; coin = rng.random((2, 4 * I)) < 0.5
    z[0:2, 7, 7] = np.where(inner & coin, 254, 255); z[0:2, 7, 15] = np.where(inner & ~coin, 254, 255)
    h = np.arange(P >> 1); seq = np.stack([h, P - 1 - h], axis=1).reshape(I, M)
    lan = np.argsort(rng.random((N, 4, 4, I)), axis=-1)
    lan[:, :, 0] = np.concatenate([1 + np.argsort(rng.random((N, 4, I - 1)), axis=-1), np.zeros((N, 4, 1), np.int64)], axis=-1)
    mem = lists(rng); mem[:, 0::2] = seq[lan].reshape(N, 4, 4, P)
    return pack(x, w, z, mem)
def setup_inputs_corners(rng):
    x, w, z, mem = parts(rng); o = [int(a) for a in rng.permutation(8)]
    x[:, o[0]] = rng.integers(100, 101 + (RHO >> 1), (N, 16, P)); z[:, o[0]] = rng.integers(100, 101 + (RHO >> 1), (N, 16, 4 * I))
    b = rng.integers(110, 141, (1, 16, 1)); x[:, o[1]] = b
    n = rng.choice(np.array([11, 12, 13, 16]), (N, 1, 4 * I)); pl = np.argsort(rng.random((N, 16, 4 * I)), axis=1)
    z[:, o[1]] = b + np.where(pl < n, RHO, RHO + 1) * rng.choice(np.array([-1, 1]), (N, 16, 4 * I))
    x[:, o[2]] = rng.integers(200, 256, (N, 16, P)); z[:, o[2]] = rng.integers(0, 21, (N, 16, 4 * I))
    for r in range(N):
        w[r, o[0]] = total(rng, (HALF, HALF + 1, 2 * P, 2 * P - 1)[r % 4]); w[r, o[3]] = total(rng, (2 * P + 1, 2 * P, 2 * P - 1, P)[r % 4])
        k = rng.integers(0, 4, (I, 1)); k[:4, 0] = rng.permutation(4); k[I - 1, 0] = 1 + r % 2
        twos = np.where(k == 0, 0, np.where(k == 1, (M >> 1) - 1, M >> 1))
        v = np.where(k == 3, 8, np.where(np.arange(M)[None, :] < twos, 2, 1))
        w[r, o[2], mem[r, o[2], 0]] = v.reshape(-1)
    w[:, o[4]] = 8; w[:, o[5]] = 1; w[:, o[6]] = 1; w[:, o[6], :P >> 2] = 8
    m = rng.integers(0, 3, (N, 1, 4 * I)); z[:, o[7]] = np.where(m == 0, 0, np.where(m == 1, 255, z[:, o[7]]))
    return pack(x, w, z, mem)
def setup_inputs_crowd(rng):
    x, w, z, mem = parts(rng); o = [int(a) for a in rng.permutation(8)]
    j = o.index(7 - o[0]); o[j], o[7] = o[7], o[j]
    for g in o[:5]:
        x[:, g] = rng.integers(200, 256, (N, 16, P)); z[:, g] = rng.integers(0, 21, (N, 16, 4 * I))
    w[:, o[0]] = rng.integers(2, 9, (N, P)); w[:, o[1]] = rng.integers(2, 9, (N, P)); w[:, o[2]] = 1; w[:, o[3]] = 1
    for r in range(N):
        a = int(rng.integers(0, I)); a = I - 1 if r == 0 else 0 if r == 1 else a
        z[r, o[1], :, a::I] = 227
        a = int(rng.integers(0, I)); a = I - 1 if r == N - 1 else a
        w[r, o[3], mem[r, o[3], 0, a * M:(a + 1) * M]] = 8
    mem[:, o[4], 1] = mem[:, o[4], 0].reshape(N, -1, 2, M)[:, :, ::-1].reshape(N, P)
    z[:, o[4], :, 1:I:2] = 227; w[:, o[4]] = np.minimum(rng.geometric(0.9, (N, P)), 8)
    z[:, o[5]] = 0
    x[:, o[6]] = rng.integers(200, 256, (N, 16, P)); z[:, o[6]] = 227; w[:, o[6]] = 1
    for r in range(N):
        n = int(rng.integers(7 * I >> 4, (17 * I >> 5) + 1)); a = rng.permutation(I)[:n]
        zv = z[(r + 1) % N, o[6]]; zv[:, a] = rng.integers(0, 21, (16, n))
        wv = w[r, o[6]]; wv[mem[r, o[6], 0].reshape(I, M)[a, :M >> 4]] = 8
    x[:, o[7]] = rng.integers(200, 256, (N, 16, P)); z[:, o[7]] = rng.integers(0, 21, (N, 16, 4 * I)); w[:, o[7]] = rng.integers(2, 9, (N, P))
    z[:, o[7], :, :I] = 227; z[:, o[7], :, 2 * I:3 * I] = 227
    for r in range(1, N, 2):
        a = int(rng.integers(0, I)); a = I - 1 if r == N - 1 else 0 if r == 1 else a
        z[r, o[7], :, I + a] = 227
    return pack(x, w, z, mem)
def check_inputs(d):
    bad = []
    for k, lo, hi in (("pt", 0, 255), ("w0", 1, 8), ("z0", 0, 255), ("lm", 0, P - 1)):
        a = np.asarray(d[k]).astype(np.float64)
        if not np.all((a >= lo) & (a <= hi)): bad.append("range of " + k)
        if np.any(a != np.floor(a)): bad.append("whole numbers of " + k)
    e = np.sort(np.stack([gentries(a) for a in np.asarray(d["lm"])]).reshape(-1, P), axis=1)
    if np.any(e != np.arange(P)[None, :]): bad.append("lm: the members of a class are all different")
    return bad
def reference(pt, w0, z0, lm):
    x = pt.astype(np.float32).astype(np.int64).reshape(N, 8, 16, P); w = w0.astype(np.float32).astype(np.int64).reshape(N, 8, P)
    z = z0.astype(np.float32).astype(np.int64).reshape(N, 8, 16, 4 * I); mem = np.stack([gentries(a) for a in lm]).astype(np.int64).reshape(N, 8, 4, I, M)
    kap = KA + KB * np.arange(K); cof = 2 * np.arange(16) + 1
    A = np.zeros((N, 8), np.int64); tally = np.zeros((N, 8, RO), np.int64)
    for t in range(RO):
        c = (t % 4, (t + 1) % 4); zn = z.copy()
        for r in range(N):
            q = (r + 1 + t % (N - 1)) % N
            for g in range(8):
                zz = [z[q, g, :, a * I:(a + 1) * I] for a in c]
                wg = w[r, g].copy(); T = min(int(np.sum(wg)), 2 * P); E = np.repeat(np.arange(P), wg)[:T]
                u = np.dot(cof, zz[0])
                h = (((u[:, None] * kap[None, :]) >> 4) + 61 * np.arange(I)[:, None] + A[r, g]) & (P - 1)
                net = E[(h * (T >> 1)) >> (LG - 1)]
                p = x[r, g][:, net]
                miss = [~np.any(np.sum(np.abs(p - b[:, :, None]) <= RHO, axis=0) >= 12, axis=1) for b in zz]
                y = (np.max(p, axis=2) + np.min(p, axis=2)) >> 1
                mark = np.zeros(P, bool); heavy = 0
                for m in (0, 1):
                    sel = miss[0] if m == 0 else miss[1] & ~miss[0]
                    s = np.sum(wg[mem[r, g, c[m]]], axis=1); light = sel & (s < LIGHT)
                    mark[mem[r, g, c[m]][light]] = True; heavy = heavy + int(np.sum(sel & ~light))
                    zn[q, g, :, c[m] * I:(c[m] + 1) * I] = np.where(sel[None, :], (zz[m] + y) >> 1, zz[m])
                wg = np.where(mark, np.minimum(2 * wg, 8), wg)
                if int(np.sum(wg)) > HALF: wg = (wg + 1) >> 1
                w[r, g] = wg; A[r, g] = heavy; tally[r, g, t] = heavy
        z = zn
    return {"yw": w.astype(np.float32), "yz": z.reshape(N, 128, 4 * I).astype(np.float32).astype(BF), "ya": tally.astype(np.float32)}

@@ -1,0 +1,527 @@
+from concourse.bass import DstId, RemoteDMATransfer
+from concourse.mybir import dt, AluOpType, AxisListType, ActivationFunctionType
+
+OP = AluOpType
+AF = ActivationFunctionType
+NR = 8
+ROUNDS = 4
+BLK = 1024
+OD0, OA0, OA1, OMX, OMN = 8192, 14336, 18432, 22528, 28672
+VDIFF = (7, 9, 11, 13, 15)
+WDMA = (1, 2)
+SQ = (3,)
+
+MSG = [
+    ("i01", "z0s", 0, 256, -1, "zin0", 0), ("i2", "z0s", 256, 384, -2, "zin1", 1), ("i3", "z0s", 384, 512, -3, "zin2", 1),
+    ("u0", "zo0", 128, 256, -1, "zr1", 0), ("c0", "zo0", 0, 128, -3, "zc0", 1),
+    ("u1", "zo1", 128, 256, -1, "zr2", 0), ("f1", "zo1", 0, 128, 2, "zf1", 1),
+    ("u2", "zo2", 128, 256, -1, "zr3", 0), ("f2", "zo2", 0, 128, 3, "zf2", 1),
+    ("f3", "zo3", 0, 256, 4, "zf3", 0)]
+
+_B, _F, _I, _U = "bfloat16", "float32", "int32", "uint16"
+SCRATCH = {}
+for _n, _w, _d in [
+        ("big", 32768, _B), ("ptb", 4112, _B), ("diffp", 4096, _B), ("pE", 8192, _B), ("zeros", 8192, _B),
+        ("wrep", 4096, _B), ("sg1", 4096, _B), ("invw", 4096, _F), ("vals", 4096, _F),
+        ("zrep", 2048, _B), ("ind", 2048, _B), ("mkx", 2048, _B), ("mkn", 2048, _B),
+        ("lmI", 1024, _I), ("lm16", 1024, _U), ("inv16", 1024, _U), ("invt", 256, _F), ("invI", 256, _I),
+        ("dg", 2048, _B), ("rp", 2048, _B), ("ident", 128, _B), ("nident", 128, _B), ("bo", 128, _B), ("bot", 128, _B),
+        ("lt", 128, _B), ("bo32", 128, _F), ("lt32", 128, _F), ("one32", 128, _F), ("row0", 128, _F), ("i976", 128, _F),
+        ("kl", 384, _F), ("pI", 8, _I), ("aF", 8, _F), ("gq", 128, _F), ("orl", 128, _B), ("cb", 248, _B), ("m128", 272, _F),
+        ("wt", 256, _B), ("woff", 272, _B), ("ex", 264, _F), ("off16", 256, _U), ("w2", 256, _B), ("wf", 256, _B),
+        ("w1", 256, _F), ("smv", 8, _F), ("smi", 8, _I), ("a16", 8, _F), ("thf", 8, _F), ("yab", 4, _F), ("ywb", 256, _F),
+        ("acc", 8, _F), ("jk", 256, _B), ("zf32", 128, _F), ("z0T", 128, _B), ("dzT", 128, _B),
+        ("hI", 384, _I), ("pos16", 384, _U), ("hb0", 384, _B), ("hb1", 384, _B), ("thr", 256, _F), ("sel", 256, _F), ("nh0", 128, _F),
+        ("m1", 128, _F), ("x1", 128, _F), ("L01", 256, _B), ("mx", 128, _F), ("mn", 128, _F), ("sm", 128, _F), ("sm2", 128, _F),
+        ("q0", 128, _I), ("q1", 128, _I), ("e0", 128, _F), ("e1", 128, _F),
+        ("z0s", 512, _B), ("zin0", 256, _B), ("zin1", 128, _B), ("zin2", 128, _B), ("zr1", 128, _B), ("zr2", 128, _B),
+        ("zr3", 128, _B), ("zc0", 128, _B), ("zf1", 128, _B), ("zf2", 128, _B), ("zf3", 256, _B),
+        ("zo0", 256, _B), ("zo1", 256, _B), ("zo2", 256, _B), ("zo3", 256, _B)]:
+    SCRATCH[_n] = ("sbuf", [128, _w], _d)
+for _m in MSG:
+    SCRATCH["y_" + _m[0]] = ("sbuf", [128, _m[3] - _m[2]], _B)
+for _n, _w in [("psA", 1024), ("psB", 1024), ("psC0", 512), ("psC1", 512), ("psM", 512), ("psS", 512)]:
+    SCRATCH[_n] = ("psum", [128, _w], _F)
+
+SEMAPHORES = ["kv", "ks", "kt", "kg", "ls"] + ["d%d" % i for i in range(40)] + ["m_" + m[0] for m in MSG] + ["q_" + m[0] for m in MSG]
+
+
+def relay_of(src, dst, which, T, topo):
+    if topo.may_write(src, dst):
+        return None
+    c = [x for x in topo.cores_of(src) if x != src and T.rank_of(x) is None and topo.may_write(x, dst) and topo.may_write(src, x)]
+    near = [x for x in c if topo.die(x) == topo.die(src)]
+    c = near if near else c
+    return c[which % len(c)]
+
+
+def mask_for(src, dst, far_src, far_dst, topo):
+    m = 0
+    ok = topo.engines(src, dst)
+    for e in topo.engines(far_src, far_dst):
+        if e in ok:
+            m |= 1 << e
+    return m
+
+
+def popcount(m):
+    return bin(m).count("1")
+
+
+def rank_program(g, core, T, topo):
+    rank = T.rank_of(core)
+    cores = list(T.cores)
+    if rank is not None:
+        rank_main(g, core, rank, cores, T, topo)
+        return
+    sent = 0
+    for kind, sbuf, lo, hi, off, land, which in MSG:
+        for r in range(NR):
+            src, dst = cores[r], cores[(r + off) % NR]
+            if relay_of(src, dst, which, T, topo) == core:
+                m = mask_for(core, dst, core, dst, topo)
+                g.wait_ge(T.sem["q_" + kind], popcount(mask_for(src, core, core, dst, topo)))
+                rid, pid = topo.addr(dst, core)
+                g.remote_dma(T[land][:], T["y_" + kind][:], T.sem["m_" + kind], T.sem.ls, pid, rid, m)
+                sent += popcount(m)
+    if sent:
+        g.wait_ge(T.sem.ls, sent)
+
+
+def rank_main(g, core, rank, cores, T, topo):
+    Q = {"v": g.vector, "s": g.scalar, "t": g.tensor, "g": g, "y": g.sync}
+    SEMOF = {"v": "kv", "s": "ks", "t": "kt", "g": "kg"}
+    count = {}
+    waited = {q: {} for q in Q}
+    hist = {}
+    nd = [0]
+
+    def need(q, name, lo, hi, write, toks):
+        ps = name.startswith("ps")
+        for (l, h, wr, sem, val, qq) in hist.get(name, []):
+            if qq == q and qq in SEMOF:
+                if not (l < hi and lo < h) or not wr or (ps and q == "t"):
+                    continue
+            elif ps:
+                if l // 512 > (hi - 1) // 512 or lo // 512 > (h - 1) // 512:
+                    continue
+            elif not (l < hi and lo < h) or not (wr or write):
+                continue
+            if toks.get(sem, 0) < val:
+                toks[sem] = val
+
+    def note(name, lo, hi, write, sem, val, q):
+        L = hist.get(name, [])
+        if write:
+            L = [e for e in L if not (lo <= e[0] and e[1] <= hi)]
+        else:
+            L = [e for e in L if not (not e[2] and e[5] == q and q in SEMOF and lo <= e[0] and e[1] <= hi)]
+        L.append((lo, hi, write, sem, val, q))
+        hist[name] = L
+
+    def waits(q, reads, writes):
+        toks = {}
+        for x in reads:
+            need(q, x[1], x[2], x[3], False, toks)
+        for x in writes:
+            need(q, x[1], x[2], x[3], True, toks)
+        for sem, val in toks.items():
+            if waited[q].get(sem, 0) < val:
+                Q[q].wait_ge(T.sem[sem], val)
+                waited[q][sem] = val
+
+    def b(name, lo, hi, step=1):
+        return (T[name][:, lo:hi:step] if step != 1 else T[name][:, lo:hi], name, lo, hi)
+
+    def ap(x):
+        return x[0] if isinstance(x, tuple) else x
+
+    def emit(q, fn, reads, writes):
+        reads = [x for x in reads if isinstance(x, tuple)]
+        waits(q, reads, writes)
+        sem = SEMOF[q]
+        count[sem] = count.get(sem, 0) + 1
+        fn().then_inc(T.sem[sem], 1)
+        for x in reads:
+            note(x[1], x[2], x[3], False, sem, count[sem], q)
+        for x in writes:
+            note(x[1], x[2], x[3], True, sem, count[sem], q)
+
+    def dma(q, pairs):
+        sem = "d%d" % nd[0]
+        nd[0] += 1
+        n = 16 * len(pairs)
+        waits(q, [p[1] for p in pairs if isinstance(p[1], tuple)], [p[0] for p in pairs if isinstance(p[0], tuple)])
+        for o, i in pairs:
+            Q[q].dma_start(ap(o), ap(i)).then_inc(T.sem[sem], 16)
+        for o, i in pairs:
+            if isinstance(i, tuple):
+                note(i[1], i[2], i[3], False, sem, n, q + "dma")
+        for o, i in pairs:
+            if isinstance(o, tuple):
+                note(o[1], o[2], o[3], True, sem, n, q + "dma")
+        count[sem] = n
+
+    def tt(o, x, y, op):
+        emit("v", lambda: g.vector.tensor_tensor(o[0], x[0], y[0], op), [x, y], [o])
+
+    def ts(o, x, s1, op0, s2=None, op1=None):
+        if op1 is None:
+            emit("v", lambda: g.vector.tensor_scalar(o[0], x[0], ap(s1), None, op0), [x, s1], [o])
+        else:
+            emit("v", lambda: g.vector.tensor_scalar(o[0], x[0], ap(s1), ap(s2), op0, op1), [x, s1, s2], [o])
+
+    def cp(o, x):
+        emit("v", lambda: g.vector.tensor_copy(o[0], x[0]), [x], [o])
+
+    def ms(o, c):
+        emit("v", lambda: g.vector.memset(o[0], c), [], [o])
+
+    def red(o, x):
+        emit("v", lambda: g.vector.tensor_reduce(o[0], x[0], AxisListType.X, OP.add), [x], [o])
+
+    def scan(o, d0, d1, op0, op1):
+        emit("v", lambda: g.vector.tensor_tensor_scan(o[0], d0[0], d1[0], 0.0, op0, op1), [d0, d1], [o])
+
+    def act(o, x, func, bias=0.0, scale=1.0):
+        emit("s", lambda: g.scalar.activation(o[0], x[0], func, bias=bias, scale=ap(scale)), [x, scale], [o])
+
+    def total(o, x):
+        j = b("jk", 0, 256)
+        emit("s", lambda: g.scalar.activation(j[0], x[0], AF.Copy, accum_out=o[0]), [x], [j, o])
+
+    def mm(o, l, r, start, stop):
+        emit("t", lambda: g.tensor.matmul(o[0], l[0], r[0], start, stop), [l, r], [o])
+
+    def asel(o, i, pattern, op, base, cm):
+        emit("g", lambda: g.affine_select(o[0], i[0], pattern, op, 0.0, base, cm), [i], [o])
+
+    def iota(o, pattern, base, cm, flag=True):
+        if flag:
+            emit("g", lambda: g.iota(o[0], pattern, base, cm, allow_small_or_imprecise_dtypes=True), [], [o])
+        else:
+            emit("g", lambda: g.iota(o[0], pattern, base, cm), [], [o])
+
+    def gath(q, o, win, off):
+        if q == "s":
+            emit("s", lambda: g.scalar.activation(o[0], win[0].indirect(off[0]), AF.Copy), [win, off], [o])
+        else:
+            emit("v", lambda: g.vector.tensor_copy(o[0], win[0].indirect(off[0])), [win, off], [o])
+
+    for kind, sbuf, lo, hi, off, land, which in MSG:
+        src = cores[(rank - off) % NR]
+        rel = relay_of(src, core, which, T, topo)
+        far = src if rel is None else rel
+        count["m_" + kind] = popcount(mask_for(far, core, far, core, topo))
+        note(land, 0, hi - lo, True, "m_" + kind, count["m_" + kind], "net")
+
+    def send(kind):
+        for k, sbuf, lo, hi, off, land, which in MSG:
+            if k == kind:
+                dst = cores[(rank + off) % NR]
+                rel = relay_of(core, dst, which, T, topo)
+                src = b(sbuf, lo, hi)
+                waits("g", [src], [])
+                if rel is None:
+                    m, to, out, sem = mask_for(core, dst, core, dst, topo), dst, T[land][:], "m_" + kind
+                else:
+                    m, to, out, sem = mask_for(core, rel, rel, dst, topo), rel, T["y_" + kind][:], "q_" + kind
+                rid, pid = topo.addr(to, core)
+                g.remote_dma(out, src[0], T.sem[sem], T.sem.ls, pid, rid, m)
+                count["ls"] = count.get("ls", 0) + popcount(m)
+
+    dma("y", [(b("wt", 0, 256), T.w0[:])])
+    dma("s", [(b("z0s", 0, 512), T.z0[:])])
+    for k in range(4):
+        dma("y", [(b("ptb", 16 + 1024 * k, 1040 + 1024 * k), T.pt[:, 1024 * k:1024 * k + 1024])])
+    dma("y", [(b("lmI", 0, 1024), T.lm[:])])
+    ms(b("zrep", 0, 2048), 1.0)
+    ms(b("ptb", 0, 16), 0.0)
+    ms(b("one32", 0, 128), 1.0)
+    ms(b("m128", 0, 272), -128.0)
+    ms(b("woff", 0, 8), 128.0)
+    ms(b("a16", 0, 8), 0.0)
+    ms(b("cb", 0, 248), 0.0)
+
+    iota(b("pI", 0, 1), [[0, 1]], 0, 1, False)
+    asel(b("ident", 0, 128), b("zrep", 0, 128), [[-1, 128]], OP.is_equal, 0, 1)
+    asel(b("bot", 0, 128), b("zrep", 0, 128), [[-16, 8], [0, 16]], OP.is_ge, 0, 1)
+    asel(b("bo", 0, 128), b("bot", 0, 128), [[16, 8], [0, 16]], OP.is_ge, 15, -1)
+    asel(b("lt", 0, 128), b("bo", 0, 128), [[1, 128]], OP.is_ge, -1, -1)
+    ts(b("nident", 0, 128), b("ident", 0, 128), -1.0, OP.mult)
+    send("i01")
+    asel(b("rp", 0, 2048), b("zrep", 0, 2048), [[-1, 16], [-16, 8], [0, 16]], OP.is_equal, 0, 1)
+    send("i2")
+    send("i3")
+    kl = b("kl", 0, 384)
+    iota(kl, [[80, 3], [0, 8], [5, 16]], 17, 0)
+    asel(kl, kl, [[0, 3], [-16, 8], [0, 16]], OP.is_ge, 0, 1)
+    asel(kl, kl, [[0, 3], [16, 8], [0, 16]], OP.is_ge, 15, -1)
+    asel(b("row0", 0, 128), b("one32", 0, 128), [[0, 128]], OP.is_equal, 0, 1)
+    iota(b("i976", 0, 128), [[976, 128]], 0, 0)
+    iota(b("vals", 0, 4096), [[1, 128], [0, 32]], 64, 0)
+    asel(b("ind", 0, 2048), b("zrep", 0, 2048), [[-1, 128], [0, 16]], OP.is_equal, 0, 1)
+    iota(b("gq", 0, 128), [[1, 8], [0, 16]], 0, 0)
+    asel(b("dg", 0, 2048), b("rp", 0, 2048), [[-1, 16], [0, 8], [1, 16]], OP.is_equal, 0, 0)
+    iota(b("zeros", 0, 8192), [[0, 8192]], 0, 0)
+
+    ms(b("big", 0, 8192), 0.0)
+    cp(b("bo32", 0, 128), b("bo", 0, 128))
+    cp(b("lt32", 0, 128), b("lt", 0, 128))
+    ts(b("woff", 8, 264), b("wt", 0, 256), 128.0, OP.add)
+
+    def prefix_scan():
+        scan(b("ex", 0, 257), b("m128", 0, 257), b("woff", 7, 264), OP.add, OP.add)
+
+    def prefix_end():
+        mm(b("psM", 1, 2), b("lt32", 0, 128), b("ex", 256, 257), True, True)
+        mm(b("psM", 2, 3), b("bo32", 0, 128), b("ex", 256, 257), True, True)
+        ts(b("off16", 0, 256), b("ex", 0, 256), b("psM", 1, 2), OP.add)
+
+    prefix_scan()
+    banks = (("psA", 0), ("psA", 512), ("psB", 0), ("psB", 512), ("psC0", 0), ("psC1", 0))
+    for a in range(16):
+        p = b(banks[a % 6][0], banks[a % 6][1], banks[a % 6][1] + 256)
+        o = b("diffp", a, 4096, 16)
+        mm(p, b("ident", 0, 128), b("ptb", 16 + 256 * a, 272 + 256 * a), True, False)
+        mm(p, b("nident", 0, 128), b("ptb", 15 + 256 * a, 271 + 256 * a), False, True)
+        if a in VDIFF:
+            ts(o, p, 0.5, OP.mult)
+        else:
+            act(o, p, AF.Copy, 0.0, 0.5)
+    prefix_end()
+    cp(b("lm16", 0, 256), b("lmI", 0, 256))
+    ts(b("pI", 1, 2), b("pI", 0, 1), 15, OP.bitwise_and)
+    ts(b("aF", 2, 3), b("pI", 1, 2), 2.0, OP.mult, 1.0, OP.add)
+
+    def later_constants():
+        cp(b("lm16", 256, 1024), b("lmI", 256, 1024))
+        ts(b("pI", 2, 3), b("pI", 0, 1), 7, OP.bitwise_and)
+        cp(b("aF", 1, 2), b("pI", 2, 3))
+        ts(b("orl", 0, 128), b("gq", 0, 128), b("aF", 1, 2), OP.is_equal)
+        cp(b("cb", 120, 128), b("bo", 0, 128, 16))
+        ms(b("mkx", 0, 2048), 512.0)
+        ms(b("mkn", 0, 2048), -512.0)
+        ms(b("mkx", 0, 2048, 16), -512.0)
+        ms(b("mkn", 0, 2048, 16), 512.0)
+
+    def inverse(c, k, n):
+        m = 4096 // n
+        w, v, off = b("invw", 0, 4096), b("vals", m * k, m * k + m), b("lm16", 256 * c + m // 16 * k, 256 * c + m // 16 * (k + 1))
+        emit("s", lambda: g.scalar.activation(w[0].indirect(off[0]), v[0], AF.Silu), [v, off], [w])
+
+    def inverse_table():
+        dma("y", [((T.invt[a::16, 0:256], "invt", 0, 256), (T.invw[a::16, 256 * a:256 * a + 256], "invw", 0, 4096)) for a in range(16)])
+
+    def inverse_list(c):
+        ts(b("invI", 0, 256), b("invt", 0, 256), -64.0, OP.add)
+        cp(b("inv16", 256 * c, 256 * c + 256), b("invI", 0, 256))
+
+    ZSRC = [(("zin0", 0), ("zin0", 128)), (("zr1", 0), ("zin1", 0)), (("zr2", 0), ("zin2", 0)), (("zr3", 0), ("zc0", 0))]
+    MB, MO = ("ptb", "sg1"), (16, 0)
+    for t in range(ROUNDS):
+        c0, c1 = t % 4, (t + 1) % 4
+        last = t == ROUNDS - 1
+        z0 = b(ZSRC[t][0][0], ZSRC[t][0][1], ZSRC[t][0][1] + 128)
+        z1 = b(ZSRC[t][1][0], ZSRC[t][1][1], ZSRC[t][1][1] + 128)
+        bigw, offs, dif = b("big", 0, 32768), b("off16", 0, 256), b("diffp", 0, 4096)
+        emit("v", lambda: g.vector.tensor_copy(bigw[0].indirect(offs[0]), dif[0]), [dif, offs], [bigw])
+        if t in WDMA:
+            dma("y", [((T.wrep[a::16, :], "wrep", 0, 4096), b("woff", 8, 264)) for a in range(16)])
+            inverse_table()
+        else:
+            for q in range(4):
+                ps = ("psA", "psB")[q % 2]
+                for k in range(4):
+                    a = 4 * q + k
+                    mm(b(ps, 256 * k, 256 * k + 256), b("rp", 128 * a, 128 * a + 128), b("woff", 8, 264), True, True)
+                act(b("wrep", 1024 * q, 1024 * q + 1024), b(ps, 0, 1024), AF.Copy)
+        if t == 0:
+            act(kl, kl, AF.Copy, 0.0, b("aF", 2, 3))
+        gath("s", b("ptb", 16, 4112), b("wrep", 0, 4096), b("lm16", 256 * c0, 256 * c0 + 256))
+        if t == 0:
+            inverse(0, 0, 1)
+        act(b("zf32", 0, 128), z0, AF.Copy)
+        mm(b("psC1", 0, 128), z0, b("ident", 0, 128), True, True)
+        mm(b("psC1", 128, 256), z0, b("ident", 0, 128), True, False)
+        mm(b("psC1", 128, 256), z1, b("nident", 0, 128), False, True)
+        for k2 in range(3):
+            p = b("psC0", 128 * k2, 128 * k2 + 128)
+            mm(p, b("kl", 128 * k2, 128 * k2 + 128), b("zf32", 0, 128), True, False)
+            mm(p, b("row0", 0, 128), b("i976", 0, 128), False, True)
+        act(b("z0T", 0, 128), b("psC1", 0, 128), AF.Copy)
+        act(b("dzT", 0, 128), b("psC1", 128, 256), AF.Copy)
+        for q in range(4):
+            mm(b(("psA", "psB")[q // 2], 512 * (q % 2), 512 * (q % 2) + 512), b("z0T", 0, 128), b("ind", 512 * q, 512 * q + 512), True, True)
+        act(b("zrep", 0, 1024), b("psA", 0, 1024), AF.Copy)
+        act(b("zrep", 1024, 2048), b("psB", 0, 1024), AF.Copy)
+        for i in range(32):
+            mm(b("psS", 0, 128), b("ident", 0, 128), b("ptb", 16 + i, 4112, 32), i == 0, i == 31)
+        if t == 0:
+            inverse_table()
+            later_constants()
+        ts(b("smi", 0, 1), b("psM", 2, 3), 0.5, OP.mult, -0.25, OP.add)
+        ts(b("thf", 0, 1), b("smi", 0, 1), 4096.0, OP.min)
+
+        def heavy(r):
+            ts(b("smv", 4, 5), b("acc", 1, 2), -16.0, OP.mult)
+            ts(b("a16", 0, 1), b("acc", 0, 1), 16.0, OP.mult, b("smv", 4, 5), OP.add)
+            ts(b("yab", r, r + 1), b("a16", 0, 1), 0.0625, OP.mult)
+
+        if t > 0:
+            heavy(t - 1)
+        scan(b("pE", 0, 8192), b("big", 0, 8192), b("big", 0, 8192), OP.add, OP.add)
+        if not last:
+            dma("y", [(b("big", 0, 8192), b("zeros", 0, 8192))])
+        else:
+            dma("y", [(T.yz[:, 128:256], b("zf1", 0, 128)), (T.yz[:, 256:384], b("zf2", 0, 128))])
+        for k in range(4):
+            mm(b("psM", 384, 512), b(("ident", "nident")[k // 2], 0, 128), (z0, z1)[k // 2], k == 0, k == 3)
+        if t == 0:
+            gath("v", b("sg1", 0, 4096), b("wrep", 0, 4096), b("lm16", 256 * c1, 256 * c1 + 256))
+        hI = b("hI", 0, 384)
+        ts(hI, b("psC0", 0, 384), b("a16", 0, 1), OP.add)
+        ts(hI, hI, 4, OP.arith_shift_right, 4095, OP.bitwise_and)
+        ts(hI, hI, b("thf", 0, 1), OP.mult)
+        ts(hI, hI, 11, OP.arith_shift_right)
+        cp(b("pos16", 0, 384), hI)
+
+        def ring(m, bk, lo=0, step=1):
+            base = (OA0, OA1)[m] + BLK * (bk % 4)
+            return b("big", base + lo, base + BLK, step)
+
+        def gather(bk):
+            o, win, off = b("big", OD0 + bk * BLK, OD0 + bk * BLK + BLK), b("pE", 0, 8192), b("pos16", 64 * bk, 64 * bk + 64)
+            zz = b("zrep", BLK * (bk % 2), BLK * (bk % 2) + BLK)
+            emit("v", lambda: g.vector.tensor_tensor(o[0], win[0].indirect(off[0]), zz[0], OP.subtract), [win, off, zz], [o])
+            act(ring(0, bk), o, AF.Abs)
+            ps = ("psA", "psB")[bk % 2]
+            for h in range(2):
+                p = b(ps, 512 * h, 512 * h + 512)
+                mm(p, b("ident", 0, 128), b("big", OD0 + bk * BLK + 512 * h, OD0 + bk * BLK + 512 * h + 512), True, False)
+                mm(p, b("dzT", 0, 128), b("ind", BLK * (bk % 2) + 512 * h, BLK * (bk % 2) + 512 * h + 512), False, True)
+            act(ring(1, bk), b(ps, 0, 1024), AF.Abs)
+            if bk < 4:
+                if t == 0:
+                    inverse(1, bk, 4)
+                else:
+                    gath("s", b("sg1", BLK * bk, BLK * bk + BLK), b("wrep", 0, 4096), b("lm16", 256 * c1 + 64 * bk, 256 * c1 + 64 * bk + 64))
+
+        def compare(bk):
+            k2, half = bk // 2, bk % 2
+            for m in range(2):
+                ts(ring(m, bk), ring(m, bk), 68.0, OP.is_le)
+                for a in range(16):
+                    mm(b("psC%d" % m, 128 * k2 + 64 * half, 128 * k2 + 64 * half + 64), b("cb", 120 - 8 * a, 248 - 8 * a),
+                       ring(m, bk, a, 16), a == 0, a == 15)
+
+        MXB = (("big", OMX), ("big", OMX + 2048), ("big", OMX + 4096))
+        MNB = (("big", OMN), ("big", OMN + 2048), ("pE", 0))
+
+        def extremes(k2):
+            d = b("big", OD0 + 2048 * k2, OD0 + 2048 * k2 + 2048)
+            scan(b(MXB[k2][0], MXB[k2][1], MXB[k2][1] + 2048), b("mkx", 0, 2048), d, OP.min, OP.max)
+            scan(b(MNB[k2][0], MNB[k2][1], MNB[k2][1] + 2048), b("mkn", 0, 2048), d, OP.max, OP.min)
+
+        gather(0)
+        gather(1)
+        gather(2)
+        if t == 0:
+            inverse_list(0)
+        compare(0)
+        extremes(0)
+        gather(3)
+        compare(1)
+        gather(4)
+        compare(2)
+        extremes(1)
+        gather(5)
+        for i in range(32):
+            mm(b("psS", 128, 256), b("ident", 0, 128), b("sg1", i, 4096, 32), i == 0, i == 31)
+        compare(3)
+        if t in (1, 2):
+            inverse_list(t + 1)
+        if t == 0:
+            inverse_table()
+        compare(4)
+        extremes(2)
+        ts(b("thr", 0, 256), b("psS", 0, 256), 4143.5, OP.is_lt, 0.5, OP.mult)
+        compare(5)
+        hits = (b("psM", 128, 256), b("psS", 256, 384))
+        for m in range(2):
+            act(b("hb%d" % m, 0, 384), b("psC%d" % m, 0, 384), AF.Relu, -11.0)
+            for k2 in range(3):
+                mm(hits[m], b("orl", 0, 128), b("hb%d" % m, 128 * k2, 128 * k2 + 128), k2 == 0, k2 == 2)
+        tt(b("L01", 0, 128), hits[0], b("thr", 0, 128), OP.is_lt)
+        ts(b("nh0", 0, 128), hits[0], 0.5, OP.is_ge)
+        tt(b("x1", 0, 128), hits[1], b("thr", 128, 256), OP.is_lt)
+        tt(b("L01", 128, 256), b("x1", 0, 128), b("nh0", 0, 128), OP.mult)
+
+        def mark_gather(q, m, k):
+            c = (c0, c1)[m]
+            gath(q, b(MB[m], MO[m] + 1024 * k, MO[m] + 1024 * k + 1024), b("L01", 128 * m, 128 * m + 128),
+                 b("inv16", 256 * c + 64 * k, 256 * c + 64 * k + 64))
+
+        def centres():
+            for buf, o, op in ((MXB, "mx", OP.max), (MNB, "mn", OP.min)):
+                e = [b(n, lo + 15, lo + 2048, 16) for n, lo in buf]
+                tt(b(o, 0, 128), e[0], e[1], op)
+                tt(b(o, 0, 128), b(o, 0, 128), e[2], op)
+            ts(b("sel", 0, 128), hits[0], 0.5, OP.is_lt)
+            ts(b("m1", 0, 128), hits[1], 0.5, OP.is_lt)
+            tt(b("sel", 128, 256), b("m1", 0, 128), b("nh0", 0, 128), OP.mult)
+            tt(b("sm", 0, 128), b("mx", 0, 128), b("mn", 0, 128), OP.add)
+            tt(b("sm2", 0, 128), b("psM", 384, 512), b("sm", 0, 128), OP.add)
+            ts(b("q0", 0, 128), b("sm", 0, 128), 0.25, OP.mult, -0.375, OP.add)
+            ts(b("q1", 0, 128), b("sm2", 0, 128), 0.25, OP.mult, -0.375, OP.add)
+            tt(b("e0", 0, 128), b("q0", 0, 128), b("sel", 0, 128), OP.mult)
+            tt(b("e1", 0, 128), b("q1", 0, 128), b("sel", 128, 256), OP.mult)
+            tt(b("zo%d" % t, 128, 256), b("e1", 0, 128), z1, OP.add)
+            tt(b("zo%d" % t, 0, 128), b("e0", 0, 128), z0, OP.add)
+            for kind in (("u0", "c0"), ("u1", "f1"), ("u2", "f2"), ("f3",))[t]:
+                send(kind)
+
+        if t == 0:
+            ts(b("dg", 0, 2048), b("dg", 0, 2048), 8.0, OP.mult)
+            inverse_list(1)
+        for k in range(4):
+            mark_gather("s", 0, k)
+        if last:
+            centres()
+        for k in range(4):
+            mark_gather("s" if k in SQ else "v", 1, k)
+        if not last:
+            centres()
+        total(b("acc", 0, 1), b("sel", 0, 256))
+        total(b("acc", 1, 2), b("L01", 0, 256))
+        if t < 2:
+            inverse(t + 2, 0, 1)
+        ts(b("wf", 0, 256), b("woff", 8, 264), -128.0, OP.add)
+        ts(b("w2", 0, 256), b("wf", 0, 256), 2.0, OP.mult, 8.0, OP.min)
+        for h in range(2):
+            p = b("psA", 512 * h, 512 * h + 128)
+            for m in range(2):
+                for a in range(16):
+                    mm(p, b("dg", 128 * a, 128 * a + 128), b(MB[m], MO[m] + 2048 * h + a, MO[m] + 2048 * h + 2048, 16),
+                       m == 0 and a == 0, m == 1 and a == 15)
+            w1 = b("w1", 128 * h, 128 * h + 128)
+            tt(w1, p, b("w2", 128 * h, 128 * h + 128), OP.min)
+            tt(w1, w1, b("wf", 128 * h, 128 * h + 128), OP.max)
+        red(b("smv", 0, 1), b("w1", 0, 256))
+        mm(b("psM", 0, 1), b("bo32", 0, 128), b("smv", 0, 1), True, True)
+        ts(b("smv", 1, 2), b("psM", 0, 1), 7168.5, OP.is_gt, -0.5, OP.mult)
+        ts(b("smv", 2, 3), b("smv", 1, 2), 1.0, OP.add)
+        ts(b("smv", 3, 4), b("smv", 1, 2), -0.5, OP.mult, 128.0, OP.add)
+        ts(b("woff", 8, 264), b("w1", 0, 256), b("smv", 2, 3), OP.mult, b("smv", 3, 4), OP.add)
+        if not last:
+            prefix_scan()
+            prefix_end()
+
+    ts(b("ywb", 0, 256), b("woff", 8, 264), -128.0, OP.add)
+    dma("y", [(T.yw[:], b("ywb", 0, 256))])
+    heavy(ROUNDS - 1)
+    dma("y", [(T.ya[:], (T.yab[0::16, 0:4], "yab", 0, 4))])
+    dma("s", [(T.yz[:, 384:512], b("zf3", 0, 128)), (T.yz[:, 0:128], b("zf3", 128, 256))])
+    for sem, val in count.items():
+        if waited["g"].get(sem, 0) < val:
+            g.wait_ge(T.sem[sem], val)

@@ -7,9 +7,8 @@ NR = 8
 ROUNDS = 4
 BLK = 1024
 OD0, OA0, OA1, OMX, OMN = 8192, 14336, 18432, 22528, 28672
-VDIFF = (7, 9, 11, 13, 15)
 WDMA = (1, 2)
-SQ = (3,)
+VO = (0, 1, 2, 3)
 
 MSG = [
     ("i01", "z0s", 0, 256, -1, "zin0", 0), ("i2", "z0s", 256, 384, -2, "zin1", 1), ("i3", "z0s", 384, 512, -3, "zin2", 1),
@@ -22,18 +21,17 @@ _B, _F, _I, _U = "bfloat16", "float32", "int32", "uint16"
 SCRATCH = {}
 for _n, _w, _d in [
         ("big", 32768, _B), ("ptb", 4112, _B), ("diffp", 4096, _B), ("pE", 8192, _B), ("zeros", 8192, _B),
-        ("wrep", 4096, _B), ("sg1", 4096, _B), ("invw", 4096, _F), ("vals", 4096, _F),
+        ("wrep", 4096, _B), ("b0r", 2048, _B), ("sg1", 4096, _B), ("invw", 4096, _F), ("vals", 4096, _F),
         ("zrep", 2048, _B), ("ind", 2048, _B), ("mkx", 2048, _B), ("mkn", 2048, _B),
-        ("lmI", 1024, _I), ("lm16", 1024, _U), ("inv16", 1024, _U), ("invt", 256, _F), ("invI", 256, _I),
+        ("lmI", 1024, _I), ("lm16", 1024, _U), ("inv16", 1024, _U), ("invt", 256, _F),
         ("dg", 2048, _B), ("rp", 2048, _B), ("ident", 128, _B), ("nident", 128, _B), ("bo", 128, _B), ("bot", 128, _B),
         ("lt", 128, _B), ("bo32", 128, _F), ("lt32", 128, _F), ("one32", 128, _F), ("row0", 128, _F), ("i976", 128, _F),
-        ("kl", 384, _F), ("pI", 8, _I), ("aF", 8, _F), ("gq", 128, _F), ("orl", 128, _B), ("cb", 248, _B), ("m128", 272, _F),
-        ("wt", 256, _B), ("woff", 272, _B), ("ex", 264, _F), ("off16", 256, _U), ("w2", 256, _B), ("wf", 256, _B),
+        ("kl", 384, _F), ("pI", 8, _I), ("aF", 8, _F), ("gq", 128, _F), ("orl", 128, _B), ("cb", 248, _B), ("ncb", 248, _B),
+        ("m128", 272, _F), ("wt", 256, _B), ("woff", 272, _B), ("ex", 264, _F), ("off16", 256, _U), ("w2", 256, _B), ("wf", 256, _B),
         ("w1", 256, _F), ("smv", 8, _F), ("smi", 8, _I), ("a16", 8, _F), ("thf", 8, _F), ("yab", 4, _F), ("ywb", 256, _F),
         ("acc", 8, _F), ("jk", 256, _B), ("zf32", 128, _F), ("z0T", 128, _B), ("dzT", 128, _B),
         ("hI", 384, _I), ("pos16", 384, _U), ("hb0", 384, _B), ("hb1", 384, _B), ("thr", 256, _F), ("sel", 256, _F), ("nh0", 128, _F),
-        ("m1", 128, _F), ("x1", 128, _F), ("L01", 256, _B), ("mx", 128, _F), ("mn", 128, _F), ("sm", 128, _F), ("sm2", 128, _F),
-        ("q0", 128, _I), ("q1", 128, _I), ("e0", 128, _F), ("e1", 128, _F),
+        ("m1", 128, _F), ("x1", 128, _F), ("L01", 256, _B), ("mx", 128, _B), ("mn", 128, _B), ("q01", 256, _I), ("e01", 256, _B),
         ("z0s", 512, _B), ("zin0", 256, _B), ("zin1", 128, _B), ("zin2", 128, _B), ("zr1", 128, _B), ("zr2", 128, _B),
         ("zr3", 128, _B), ("zc0", 128, _B), ("zf1", 128, _B), ("zf2", 128, _B), ("zf3", 256, _B),
         ("zo0", 256, _B), ("zo1", 256, _B), ("zo2", 256, _B), ("zo3", 256, _B)]:
@@ -259,9 +257,9 @@ def rank_main(g, core, rank, cores, T, topo):
     asel(kl, kl, [[0, 3], [16, 8], [0, 16]], OP.is_ge, 15, -1)
     asel(b("row0", 0, 128), b("one32", 0, 128), [[0, 128]], OP.is_equal, 0, 1)
     iota(b("i976", 0, 128), [[976, 128]], 0, 0)
+    iota(b("gq", 0, 128), [[1, 8], [0, 16]], 0, 0)
     iota(b("vals", 0, 4096), [[1, 128], [0, 32]], 64, 0)
     asel(b("ind", 0, 2048), b("zrep", 0, 2048), [[-1, 128], [0, 16]], OP.is_equal, 0, 1)
-    iota(b("gq", 0, 128), [[1, 8], [0, 16]], 0, 0)
     asel(b("dg", 0, 2048), b("rp", 0, 2048), [[-1, 16], [0, 8], [1, 16]], OP.is_equal, 0, 0)
     iota(b("zeros", 0, 8192), [[0, 8192]], 0, 0)
 
@@ -273,37 +271,33 @@ def rank_main(g, core, rank, cores, T, topo):
     def prefix_scan():
         scan(b("ex", 0, 257), b("m128", 0, 257), b("woff", 7, 264), OP.add, OP.add)
 
-    def prefix_end():
+    def prefix_sums():
         mm(b("psM", 1, 2), b("lt32", 0, 128), b("ex", 256, 257), True, True)
         mm(b("psM", 2, 3), b("bo32", 0, 128), b("ex", 256, 257), True, True)
+
+    def prefix_end():
         ts(b("off16", 0, 256), b("ex", 0, 256), b("psM", 1, 2), OP.add)
 
     prefix_scan()
     banks = (("psA", 0), ("psA", 512), ("psB", 0), ("psB", 512), ("psC0", 0), ("psC1", 0))
     for a in range(16):
         p = b(banks[a % 6][0], banks[a % 6][1], banks[a % 6][1] + 256)
-        o = b("diffp", a, 4096, 16)
         mm(p, b("ident", 0, 128), b("ptb", 16 + 256 * a, 272 + 256 * a), True, False)
         mm(p, b("nident", 0, 128), b("ptb", 15 + 256 * a, 271 + 256 * a), False, True)
-        if a in VDIFF:
-            ts(o, p, 0.5, OP.mult)
-        else:
-            act(o, p, AF.Copy, 0.0, 0.5)
+        act(b("diffp", a, 4096, 16), p, AF.Copy, 0.0, 0.5)
+    ms(b("mkx", 0, 2048), 512.0)
+    ms(b("mkn", 0, 2048), -512.0)
+    ms(b("mkx", 0, 2048, 16), -512.0)
+    ms(b("mkn", 0, 2048, 16), 512.0)
+    cp(b("lm16", 0, 1024), b("lmI", 0, 1024))
+    cp(b("cb", 120, 128), b("bo", 0, 128, 16))
+    ts(b("ncb", 0, 248), b("cb", 0, 248), -1.0, OP.mult)
+    prefix_sums()
     prefix_end()
-    cp(b("lm16", 0, 256), b("lmI", 0, 256))
+    ts(b("pI", 2, 3), b("pI", 0, 1), 7, OP.bitwise_and)
+    cp(b("aF", 1, 2), b("pI", 2, 3))
     ts(b("pI", 1, 2), b("pI", 0, 1), 15, OP.bitwise_and)
     ts(b("aF", 2, 3), b("pI", 1, 2), 2.0, OP.mult, 1.0, OP.add)
-
-    def later_constants():
-        cp(b("lm16", 256, 1024), b("lmI", 256, 1024))
-        ts(b("pI", 2, 3), b("pI", 0, 1), 7, OP.bitwise_and)
-        cp(b("aF", 1, 2), b("pI", 2, 3))
-        ts(b("orl", 0, 128), b("gq", 0, 128), b("aF", 1, 2), OP.is_equal)
-        cp(b("cb", 120, 128), b("bo", 0, 128, 16))
-        ms(b("mkx", 0, 2048), 512.0)
-        ms(b("mkn", 0, 2048), -512.0)
-        ms(b("mkx", 0, 2048, 16), -512.0)
-        ms(b("mkn", 0, 2048, 16), 512.0)
 
     def inverse(c, k, n):
         m = 4096 // n
@@ -314,11 +308,13 @@ def rank_main(g, core, rank, cores, T, topo):
         dma("y", [((T.invt[a::16, 0:256], "invt", 0, 256), (T.invw[a::16, 256 * a:256 * a + 256], "invw", 0, 4096)) for a in range(16)])
 
     def inverse_list(c):
-        ts(b("invI", 0, 256), b("invt", 0, 256), -64.0, OP.add)
-        cp(b("inv16", 256 * c, 256 * c + 256), b("invI", 0, 256))
+        ts(b("inv16", 256 * c, 256 * c + 256), b("invt", 0, 256), -63.75, OP.add)
 
     ZSRC = [(("zin0", 0), ("zin0", 128)), (("zr1", 0), ("zin1", 0)), (("zr2", 0), ("zin2", 0)), (("zr3", 0), ("zc0", 0))]
     MB, MO = ("ptb", "sg1"), (16, 0)
+    MP = (("psA", 0), ("psA", 512), ("psC0", 0), ("psC1", 0))
+    MXB = (("big", OMX), ("big", OMX + 2048), ("big", OMX + 4096))
+    MNB = (("big", OMN), ("big", OMN + 2048), ("pE", 0))
     for t in range(ROUNDS):
         c0, c1 = t % 4, (t + 1) % 4
         last = t == ROUNDS - 1
@@ -341,6 +337,7 @@ def rank_main(g, core, rank, cores, T, topo):
         gath("s", b("ptb", 16, 4112), b("wrep", 0, 4096), b("lm16", 256 * c0, 256 * c0 + 256))
         if t == 0:
             inverse(0, 0, 1)
+        act(b("wf", 0, 256), b("woff", 8, 264), AF.Copy, -128.0)
         act(b("zf32", 0, 128), z0, AF.Copy)
         mm(b("psC1", 0, 128), z0, b("ident", 0, 128), True, True)
         mm(b("psC1", 128, 256), z0, b("ident", 0, 128), True, False)
@@ -359,9 +356,9 @@ def rank_main(g, core, rank, cores, T, topo):
             mm(b("psS", 0, 128), b("ident", 0, 128), b("ptb", 16 + i, 4112, 32), i == 0, i == 31)
         if t == 0:
             inverse_table()
-            later_constants()
+            ts(b("orl", 0, 128), b("gq", 0, 128), b("aF", 1, 2), OP.is_equal)
         ts(b("smi", 0, 1), b("psM", 2, 3), 0.5, OP.mult, -0.25, OP.add)
-        ts(b("thf", 0, 1), b("smi", 0, 1), 4096.0, OP.min)
+        ts(b("thf", 0, 1), b("smi", 0, 1), 4096.0, OP.min, 1.0 / 2048.0, OP.mult)
 
         def heavy(r):
             ts(b("smv", 4, 5), b("acc", 1, 2), -16.0, OP.mult)
@@ -375,16 +372,16 @@ def rank_main(g, core, rank, cores, T, topo):
             dma("y", [(b("big", 0, 8192), b("zeros", 0, 8192))])
         else:
             dma("y", [(T.yz[:, 128:256], b("zf1", 0, 128)), (T.yz[:, 256:384], b("zf2", 0, 128))])
-        for k in range(4):
-            mm(b("psM", 384, 512), b(("ident", "nident")[k // 2], 0, 128), (z0, z1)[k // 2], k == 0, k == 3)
         if t == 0:
             gath("v", b("sg1", 0, 4096), b("wrep", 0, 4096), b("lm16", 256 * c1, 256 * c1 + 256))
         hI = b("hI", 0, 384)
         ts(hI, b("psC0", 0, 384), b("a16", 0, 1), OP.add)
         ts(hI, hI, 4, OP.arith_shift_right, 4095, OP.bitwise_and)
-        ts(hI, hI, b("thf", 0, 1), OP.mult)
-        ts(hI, hI, 11, OP.arith_shift_right)
-        cp(b("pos16", 0, 384), hI)
+        ts(hI, hI, b("thf", 0, 1), OP.mult, -4095.5 + 1.0 / 4096.0, OP.add)
+        ts(b("pos16", 0, 384), hI, 4095.0, OP.add)
+
+        def two_sided(bk):
+            return t == 0 and bk in VO
 
         def ring(m, bk, lo=0, step=1):
             base = (OA0, OA1)[m] + BLK * (bk % 4)
@@ -394,7 +391,8 @@ def rank_main(g, core, rank, cores, T, topo):
             o, win, off = b("big", OD0 + bk * BLK, OD0 + bk * BLK + BLK), b("pE", 0, 8192), b("pos16", 64 * bk, 64 * bk + 64)
             zz = b("zrep", BLK * (bk % 2), BLK * (bk % 2) + BLK)
             emit("v", lambda: g.vector.tensor_tensor(o[0], win[0].indirect(off[0]), zz[0], OP.subtract), [win, off, zz], [o])
-            act(ring(0, bk), o, AF.Abs)
+            if not two_sided(bk):
+                act(ring(0, bk), o, AF.Abs)
             ps = ("psA", "psB")[bk % 2]
             for h in range(2):
                 p = b(ps, 512 * h, 512 * h + 512)
@@ -410,18 +408,31 @@ def rank_main(g, core, rank, cores, T, topo):
         def compare(bk):
             k2, half = bk // 2, bk % 2
             for m in range(2):
-                ts(ring(m, bk), ring(m, bk), 68.0, OP.is_le)
+                two = m == 0 and two_sided(bk)
+                o = b("psC%d" % m, 128 * k2 + 64 * half, 128 * k2 + 64 * half + 64)
+                lo = BLK * half
+                if two:
+                    d = b("big", OD0 + bk * BLK, OD0 + bk * BLK + BLK)
+                    ts(ring(0, bk), d, -68.0, OP.is_ge)
+                    ts(b("b0r", lo, lo + BLK), d, 68.0, OP.is_gt)
+                else:
+                    ts(ring(m, bk), ring(m, bk), 68.0, OP.is_le)
                 for a in range(16):
-                    mm(b("psC%d" % m, 128 * k2 + 64 * half, 128 * k2 + 64 * half + 64), b("cb", 120 - 8 * a, 248 - 8 * a),
-                       ring(m, bk, a, 16), a == 0, a == 15)
+                    mm(o, b("cb", 120 - 8 * a, 248 - 8 * a), ring(m, bk, a, 16), a == 0, a == 15 and not two)
+                if two:
+                    for a in range(16):
+                        mm(o, b("ncb", 120 - 8 * a, 248 - 8 * a), b("b0r", lo + a, lo + BLK, 16), False, a == 15)
 
-        MXB = (("big", OMX), ("big", OMX + 2048), ("big", OMX + 4096))
-        MNB = (("big", OMN), ("big", OMN + 2048), ("pE", 0))
-
-        def extremes(k2):
+        def extremes(k2, part=2):
             d = b("big", OD0 + 2048 * k2, OD0 + 2048 * k2 + 2048)
-            scan(b(MXB[k2][0], MXB[k2][1], MXB[k2][1] + 2048), b("mkx", 0, 2048), d, OP.min, OP.max)
-            scan(b(MNB[k2][0], MNB[k2][1], MNB[k2][1] + 2048), b("mkn", 0, 2048), d, OP.max, OP.min)
+            if part != 1:
+                scan(b(MXB[k2][0], MXB[k2][1], MXB[k2][1] + 2048), b("mkx", 0, 2048), d, OP.min, OP.max)
+            if part != 0:
+                scan(b(MNB[k2][0], MNB[k2][1], MNB[k2][1] + 2048), b("mkn", 0, 2048), d, OP.max, OP.min)
+
+        def second_sums(h):
+            for i in range(32):
+                mm(b("psS", 128 + 64 * h, 192 + 64 * h), b("ident", 0, 128), b("sg1", 2048 * h + i, 2048 * h + 2048, 32), i == 0, i == 31)
 
         gather(0)
         gather(1)
@@ -429,24 +440,25 @@ def rank_main(g, core, rank, cores, T, topo):
         if t == 0:
             inverse_list(0)
         compare(0)
-        extremes(0)
         gather(3)
         compare(1)
+        extremes(0)
+        second_sums(0)
         gather(4)
         compare(2)
-        extremes(1)
         gather(5)
-        for i in range(32):
-            mm(b("psS", 128, 256), b("ident", 0, 128), b("sg1", i, 4096, 32), i == 0, i == 31)
+        second_sums(1)
+        extremes(1)
         compare(3)
         if t in (1, 2):
             inverse_list(t + 1)
         if t == 0:
             inverse_table()
         compare(4)
-        extremes(2)
-        ts(b("thr", 0, 256), b("psS", 0, 256), 4143.5, OP.is_lt, 0.5, OP.mult)
+        extremes(2, 0)
         compare(5)
+        ts(b("thr", 0, 256), b("psS", 0, 256), 4143.5, OP.is_lt, 0.5, OP.mult)
+        extremes(2, 1)
         hits = (b("psM", 128, 256), b("psS", 256, 384))
         for m in range(2):
             act(b("hb%d" % m, 0, 384), b("psC%d" % m, 0, 384), AF.Relu, -11.0)
@@ -457,12 +469,18 @@ def rank_main(g, core, rank, cores, T, topo):
         tt(b("x1", 0, 128), hits[1], b("thr", 128, 256), OP.is_lt)
         tt(b("L01", 128, 256), b("x1", 0, 128), b("nh0", 0, 128), OP.mult)
 
-        def mark_gather(q, m, k):
+        def mark_gather(q, m, k0, k1):
             c = (c0, c1)[m]
-            gath(q, b(MB[m], MO[m] + 1024 * k, MO[m] + 1024 * k + 1024), b("L01", 128 * m, 128 * m + 128),
-                 b("inv16", 256 * c + 64 * k, 256 * c + 64 * k + 64))
+            gath(q, b(MB[m], MO[m] + 512 * k0, MO[m] + 512 * k1), b("L01", 128 * m, 128 * m + 128),
+                 b("inv16", 256 * c + 32 * k0, 256 * c + 32 * k1))
 
-        def centres():
+        def marks(m, h, first):
+            p = b(MP[h][0], MP[h][1], MP[h][1] + 64)
+            for a in range(16):
+                mm(p, b("dg", 128 * a, 128 * a + 128), b(MB[m], MO[m] + 1024 * h + a, MO[m] + 1024 * h + 1024, 16),
+                   first and a == 0, not first and a == 15)
+
+        def extremes_end():
             for buf, o, op in ((MXB, "mx", OP.max), (MNB, "mn", OP.min)):
                 e = [b(n, lo + 15, lo + 2048, 16) for n, lo in buf]
                 tt(b(o, 0, 128), e[0], e[1], op)
@@ -470,52 +488,75 @@ def rank_main(g, core, rank, cores, T, topo):
             ts(b("sel", 0, 128), hits[0], 0.5, OP.is_lt)
             ts(b("m1", 0, 128), hits[1], 0.5, OP.is_lt)
             tt(b("sel", 128, 256), b("m1", 0, 128), b("nh0", 0, 128), OP.mult)
-            tt(b("sm", 0, 128), b("mx", 0, 128), b("mn", 0, 128), OP.add)
-            tt(b("sm2", 0, 128), b("psM", 384, 512), b("sm", 0, 128), OP.add)
-            ts(b("q0", 0, 128), b("sm", 0, 128), 0.25, OP.mult, -0.375, OP.add)
-            ts(b("q1", 0, 128), b("sm2", 0, 128), 0.25, OP.mult, -0.375, OP.add)
-            tt(b("e0", 0, 128), b("q0", 0, 128), b("sel", 0, 128), OP.mult)
-            tt(b("e1", 0, 128), b("q1", 0, 128), b("sel", 128, 256), OP.mult)
-            tt(b("zo%d" % t, 128, 256), b("e1", 0, 128), z1, OP.add)
-            tt(b("zo%d" % t, 0, 128), b("e0", 0, 128), z0, OP.add)
+            one, neg, mx, mn = b("ident", 0, 128), b("nident", 0, 128), b("mx", 0, 128), b("mn", 0, 128)
+            for k, x in enumerate((mx, mn)):
+                mm(b("psB", 0, 128), one, x, k == 0, k == 1)
+            for k, (l, x) in enumerate(((one, mx), (one, mn), (one, z0), (one, z0), (neg, z1), (neg, z1))):
+                mm(b("psB", 128, 256), l, x, k == 0, k == 5)
+
+        def quarter():
+            ts(b("q01", 0, 256), b("psB", 0, 256), 0.25, OP.mult, -0.375, OP.add)
+
+        def move():
+            tt(b("e01", 0, 256), b("q01", 0, 256), b("sel", 0, 256), OP.mult)
+            for m, z in ((0, z0), (1, z1)):
+                mm(b("psB", 512 + 128 * m, 640 + 128 * m), b("ident", 0, 128), b("e01", 128 * m, 128 * m + 128), True, False)
+                mm(b("psB", 512 + 128 * m, 640 + 128 * m), b("ident", 0, 128), z, False, True)
+
+        def hand_over():
+            if t == 2:
+                act(b("zo%d" % t, 0, 256), b("psB", 512, 768), AF.Copy)
+            else:
+                cp(b("zo%d" % t, 0, 256), b("psB", 512, 768))
             for kind in (("u0", "c0"), ("u1", "f1"), ("u2", "f2"), ("f3",))[t]:
                 send(kind)
 
         if t == 0:
             ts(b("dg", 0, 2048), b("dg", 0, 2048), 8.0, OP.mult)
             inverse_list(1)
-        for k in range(4):
-            mark_gather("s", 0, k)
+        mark_gather("s", 0, 0, 4)
+        mark_gather("s", 0, 4, 8)
         if last:
-            centres()
-        for k in range(4):
-            mark_gather("s" if k in SQ else "v", 1, k)
+            extremes_end()
+            quarter()
+            move()
+            hand_over()
+        marks(0, 0, True)
+        marks(0, 1, True)
+        mark_gather("v", 1, 0, 4)
+        marks(1, 0, False)
+        marks(1, 1, False)
+        mark_gather("v", 1, 4, 6)
+        marks(1, 2, True)
+        marks(0, 2, False)
+        marks(0, 3, True)
+        mark_gather("s", 1, 6, 8)
+        marks(1, 3, False)
+        ts(b("w2", 0, 256), b("wf", 0, 256), 2.0, OP.mult, 8.0, OP.min)
         if not last:
-            centres()
+            extremes_end()
         total(b("acc", 0, 1), b("sel", 0, 256))
         total(b("acc", 1, 2), b("L01", 0, 256))
         if t < 2:
             inverse(t + 2, 0, 1)
-        ts(b("wf", 0, 256), b("woff", 8, 264), -128.0, OP.add)
-        ts(b("w2", 0, 256), b("wf", 0, 256), 2.0, OP.mult, 8.0, OP.min)
-        for h in range(2):
-            p = b("psA", 512 * h, 512 * h + 128)
-            for m in range(2):
-                for a in range(16):
-                    mm(p, b("dg", 128 * a, 128 * a + 128), b(MB[m], MO[m] + 2048 * h + a, MO[m] + 2048 * h + 2048, 16),
-                       m == 0 and a == 0, m == 1 and a == 15)
-            w1 = b("w1", 128 * h, 128 * h + 128)
-            tt(w1, p, b("w2", 128 * h, 128 * h + 128), OP.min)
-            tt(w1, w1, b("wf", 128 * h, 128 * h + 128), OP.max)
+        for h in range(4):
+            w1 = b("w1", 64 * h, 64 * h + 64)
+            tt(w1, b(MP[h][0], MP[h][1], MP[h][1] + 64), b("w2", 64 * h, 64 * h + 64), OP.min)
+            tt(w1, w1, b("wf", 64 * h, 64 * h + 64), OP.max)
         red(b("smv", 0, 1), b("w1", 0, 256))
         mm(b("psM", 0, 1), b("bo32", 0, 128), b("smv", 0, 1), True, True)
+        if not last:
+            quarter()
         ts(b("smv", 1, 2), b("psM", 0, 1), 7168.5, OP.is_gt, -0.5, OP.mult)
         ts(b("smv", 2, 3), b("smv", 1, 2), 1.0, OP.add)
         ts(b("smv", 3, 4), b("smv", 1, 2), -0.5, OP.mult, 128.0, OP.add)
         ts(b("woff", 8, 264), b("w1", 0, 256), b("smv", 2, 3), OP.mult, b("smv", 3, 4), OP.add)
         if not last:
             prefix_scan()
+            prefix_sums()
+            move()
             prefix_end()
+            hand_over()
 
     ts(b("ywb", 0, 256), b("woff", 8, 264), -128.0, OP.add)
     dma("y", [(T.yw[:], b("ywb", 0, 256))])

from concourse.bass import DstId, RemoteDMATransfer
from concourse.mybir import dt, AluOpType, AxisListType, ActivationFunctionType

OP = AluOpType
AF = ActivationFunctionType
NR = 8
ROUNDS = 4
BLK = 1024
OD0, OA0, OA1, OMX, OMN = 8192, 14336, 18432, 22528, 28672
WDMA = (1, 2)
VO = (0, 1, 2, 3)

MSG = [
    ("i01", "z0s", 0, 256, -1, "zin0", 0), ("i2", "z0s", 256, 384, -2, "zin1", 1), ("i3", "z0s", 384, 512, -3, "zin2", 1),
    ("u0", "zo0", 128, 256, -1, "zr1", 0), ("c0", "zo0", 0, 128, -3, "zc0", 1),
    ("u1", "zo1", 128, 256, -1, "zr2", 0), ("f1", "zo1", 0, 128, 2, "zf1", 1),
    ("u2", "zo2", 128, 256, -1, "zr3", 0), ("f2", "zo2", 0, 128, 3, "zf2", 1),
    ("f3", "zo3", 0, 256, 4, "zf3", 0)]

_B, _F, _I, _U = "bfloat16", "float32", "int32", "uint16"
SCRATCH = {}
for _n, _w, _d in [
        ("big", 32768, _B), ("ptb", 4112, _B), ("diffp", 4096, _B), ("pE", 8192, _B), ("zeros", 8192, _B),
        ("wrep", 4096, _B), ("b0r", 2048, _B), ("sg1", 4096, _B), ("invw", 4096, _F), ("vals", 4096, _F),
        ("zrep", 2048, _B), ("ind", 2048, _B), ("mkx", 2048, _B), ("mkn", 2048, _B),
        ("lmI", 1024, _I), ("lm16", 1024, _U), ("inv16", 1024, _U), ("invt", 256, _F),
        ("dg", 2048, _B), ("rp", 2048, _B), ("ident", 128, _B), ("nident", 128, _B), ("bo", 128, _B), ("bot", 128, _B),
        ("lt", 128, _B), ("bo32", 128, _F), ("lt32", 128, _F), ("one32", 128, _F), ("row0", 128, _F), ("i976", 128, _F),
        ("kl", 384, _F), ("pI", 8, _I), ("aF", 8, _F), ("gq", 128, _F), ("orl", 128, _B), ("cb", 248, _B), ("ncb", 248, _B),
        ("m128", 272, _F), ("wt", 256, _B), ("woff", 272, _B), ("ex", 264, _F), ("off16", 256, _U), ("w2", 256, _B), ("wf", 256, _B),
        ("w1", 256, _F), ("smv", 8, _F), ("smi", 8, _I), ("a16", 8, _F), ("thf", 8, _F), ("yab", 4, _F), ("ywb", 256, _F),
        ("acc", 8, _F), ("jk", 256, _B), ("zf32", 128, _F), ("z0T", 128, _B), ("dzT", 128, _B),
        ("hI", 384, _I), ("pos16", 384, _U), ("hb0", 384, _B), ("hb1", 384, _B), ("thr", 256, _F), ("sel", 256, _F), ("nh0", 128, _F),
        ("m1", 128, _F), ("x1", 128, _F), ("L01", 256, _B), ("mx", 128, _B), ("mn", 128, _B), ("q01", 256, _I), ("e01", 256, _B),
        ("z0s", 512, _B), ("zin0", 256, _B), ("zin1", 128, _B), ("zin2", 128, _B), ("zr1", 128, _B), ("zr2", 128, _B),
        ("zr3", 128, _B), ("zc0", 128, _B), ("zf1", 128, _B), ("zf2", 128, _B), ("zf3", 256, _B),
        ("zo0", 256, _B), ("zo1", 256, _B), ("zo2", 256, _B), ("zo3", 256, _B)]:
    SCRATCH[_n] = ("sbuf", [128, _w], _d)
for _m in MSG:
    SCRATCH["y_" + _m[0]] = ("sbuf", [128, _m[3] - _m[2]], _B)
for _n, _w in [("psA", 1024), ("psB", 1024), ("psC0", 512), ("psC1", 512), ("psM", 512), ("psS", 512)]:
    SCRATCH[_n] = ("psum", [128, _w], _F)

SEMAPHORES = ["kv", "ks", "kt", "kg", "ls"] + ["d%d" % i for i in range(40)] + ["m_" + m[0] for m in MSG] + ["q_" + m[0] for m in MSG]


def relay_of(src, dst, which, T, topo):
    if topo.may_write(src, dst):
        return None
    c = [x for x in topo.cores_of(src) if x != src and T.rank_of(x) is None and topo.may_write(x, dst) and topo.may_write(src, x)]
    near = [x for x in c if topo.die(x) == topo.die(src)]
    c = near if near else c
    return c[which % len(c)]


def mask_for(src, dst, far_src, far_dst, topo):
    m = 0
    ok = topo.engines(src, dst)
    for e in topo.engines(far_src, far_dst):
        if e in ok:
            m |= 1 << e
    return m


def popcount(m):
    return bin(m).count("1")


def rank_program(g, core, T, topo):
    rank = T.rank_of(core)
    cores = list(T.cores)
    if rank is not None:
        rank_main(g, core, rank, cores, T, topo)
        return
    sent = 0
    for kind, sbuf, lo, hi, off, land, which in MSG:
        for r in range(NR):
            src, dst = cores[r], cores[(r + off) % NR]
            if relay_of(src, dst, which, T, topo) == core:
                m = mask_for(core, dst, core, dst, topo)
                g.wait_ge(T.sem["q_" + kind], popcount(mask_for(src, core, core, dst, topo)))
                rid, pid = topo.addr(dst, core)
                g.remote_dma(T[land][:], T["y_" + kind][:], T.sem["m_" + kind], T.sem.ls, pid, rid, m)
                sent += popcount(m)
    if sent:
        g.wait_ge(T.sem.ls, sent)


def rank_main(g, core, rank, cores, T, topo):
    Q = {"v": g.vector, "s": g.scalar, "t": g.tensor, "g": g, "y": g.sync}
    SEMOF = {"v": "kv", "s": "ks", "t": "kt", "g": "kg"}
    count = {}
    waited = {q: {} for q in Q}
    hist = {}
    nd = [0]

    def need(q, name, lo, hi, write, toks):
        ps = name.startswith("ps")
        for (l, h, wr, sem, val, qq) in hist.get(name, []):
            if qq == q and qq in SEMOF:
                if not (l < hi and lo < h) or not wr or (ps and q == "t"):
                    continue
            elif ps:
                if l // 512 > (hi - 1) // 512 or lo // 512 > (h - 1) // 512:
                    continue
            elif not (l < hi and lo < h) or not (wr or write):
                continue
            if toks.get(sem, 0) < val:
                toks[sem] = val

    def note(name, lo, hi, write, sem, val, q):
        L = hist.get(name, [])
        if write:
            L = [e for e in L if not (lo <= e[0] and e[1] <= hi)]
        else:
            L = [e for e in L if not (not e[2] and e[5] == q and q in SEMOF and lo <= e[0] and e[1] <= hi)]
        L.append((lo, hi, write, sem, val, q))
        hist[name] = L

    def waits(q, reads, writes):
        toks = {}
        for x in reads:
            need(q, x[1], x[2], x[3], False, toks)
        for x in writes:
            need(q, x[1], x[2], x[3], True, toks)
        for sem, val in toks.items():
            if waited[q].get(sem, 0) < val:
                Q[q].wait_ge(T.sem[sem], val)
                waited[q][sem] = val

    def b(name, lo, hi, step=1):
        return (T[name][:, lo:hi:step] if step != 1 else T[name][:, lo:hi], name, lo, hi)

    def ap(x):
        return x[0] if isinstance(x, tuple) else x

    def emit(q, fn, reads, writes):
        reads = [x for x in reads if isinstance(x, tuple)]
        waits(q, reads, writes)
        sem = SEMOF[q]
        count[sem] = count.get(sem, 0) + 1
        fn().then_inc(T.sem[sem], 1)
        for x in reads:
            note(x[1], x[2], x[3], False, sem, count[sem], q)
        for x in writes:
            note(x[1], x[2], x[3], True, sem, count[sem], q)

    def dma(q, pairs):
        sem = "d%d" % nd[0]
        nd[0] += 1
        n = 16 * len(pairs)
        waits(q, [p[1] for p in pairs if isinstance(p[1], tuple)], [p[0] for p in pairs if isinstance(p[0], tuple)])
        for o, i in pairs:
            Q[q].dma_start(ap(o), ap(i)).then_inc(T.sem[sem], 16)
        for o, i in pairs:
            if isinstance(i, tuple):
                note(i[1], i[2], i[3], False, sem, n, q + "dma")
        for o, i in pairs:
            if isinstance(o, tuple):
                note(o[1], o[2], o[3], True, sem, n, q + "dma")
        count[sem] = n

    def tt(o, x, y, op):
        emit("v", lambda: g.vector.tensor_tensor(o[0], x[0], y[0], op), [x, y], [o])

    def ts(o, x, s1, op0, s2=None, op1=None):
        if op1 is None:
            emit("v", lambda: g.vector.tensor_scalar(o[0], x[0], ap(s1), None, op0), [x, s1], [o])
        else:
            emit("v", lambda: g.vector.tensor_scalar(o[0], x[0], ap(s1), ap(s2), op0, op1), [x, s1, s2], [o])

    def cp(o, x):
        emit("v", lambda: g.vector.tensor_copy(o[0], x[0]), [x], [o])

    def ms(o, c):
        emit("v", lambda: g.vector.memset(o[0], c), [], [o])

    def red(o, x):
        emit("v", lambda: g.vector.tensor_reduce(o[0], x[0], AxisListType.X, OP.add), [x], [o])

    def scan(o, d0, d1, op0, op1):
        emit("v", lambda: g.vector.tensor_tensor_scan(o[0], d0[0], d1[0], 0.0, op0, op1), [d0, d1], [o])

    def act(o, x, func, bias=0.0, scale=1.0):
        emit("s", lambda: g.scalar.activation(o[0], x[0], func, bias=bias, scale=ap(scale)), [x, scale], [o])

    def total(o, x):
        j = b("jk", 0, 256)
        emit("s", lambda: g.scalar.activation(j[0], x[0], AF.Copy, accum_out=o[0]), [x], [j, o])

    def mm(o, l, r, start, stop):
        emit("t", lambda: g.tensor.matmul(o[0], l[0], r[0], start, stop), [l, r], [o])

    def asel(o, i, pattern, op, base, cm):
        emit("g", lambda: g.affine_select(o[0], i[0], pattern, op, 0.0, base, cm), [i], [o])

    def iota(o, pattern, base, cm, flag=True):
        if flag:
            emit("g", lambda: g.iota(o[0], pattern, base, cm, allow_small_or_imprecise_dtypes=True), [], [o])
        else:
            emit("g", lambda: g.iota(o[0], pattern, base, cm), [], [o])

    def gath(q, o, win, off):
        if q == "s":
            emit("s", lambda: g.scalar.activation(o[0], win[0].indirect(off[0]), AF.Copy), [win, off], [o])
        else:
            emit("v", lambda: g.vector.tensor_copy(o[0], win[0].indirect(off[0])), [win, off], [o])

    for kind, sbuf, lo, hi, off, land, which in MSG:
        src = cores[(rank - off) % NR]
        rel = relay_of(src, core, which, T, topo)
        far = src if rel is None else rel
        count["m_" + kind] = popcount(mask_for(far, core, far, core, topo))
        note(land, 0, hi - lo, True, "m_" + kind, count["m_" + kind], "net")

    def send(kind):
        for k, sbuf, lo, hi, off, land, which in MSG:
            if k == kind:
                dst = cores[(rank + off) % NR]
                rel = relay_of(core, dst, which, T, topo)
                src = b(sbuf, lo, hi)
                waits("g", [src], [])
                if rel is None:
                    m, to, out, sem = mask_for(core, dst, core, dst, topo), dst, T[land][:], "m_" + kind
                else:
                    m, to, out, sem = mask_for(core, rel, rel, dst, topo), rel, T["y_" + kind][:], "q_" + kind
                rid, pid = topo.addr(to, core)
                g.remote_dma(out, src[0], T.sem[sem], T.sem.ls, pid, rid, m)
                count["ls"] = count.get("ls", 0) + popcount(m)

    dma("y", [(b("wt", 0, 256), T.w0[:])])
    dma("s", [(b("z0s", 0, 512), T.z0[:])])
    for k in range(4):
        dma("y", [(b("ptb", 16 + 1024 * k, 1040 + 1024 * k), T.pt[:, 1024 * k:1024 * k + 1024])])
    dma("y", [(b("lmI", 0, 1024), T.lm[:])])
    ms(b("zrep", 0, 2048), 1.0)
    ms(b("ptb", 0, 16), 0.0)
    ms(b("one32", 0, 128), 1.0)
    ms(b("m128", 0, 272), -128.0)
    ms(b("woff", 0, 8), 128.0)
    ms(b("a16", 0, 8), 0.0)
    ms(b("cb", 0, 248), 0.0)

    iota(b("pI", 0, 1), [[0, 1]], 0, 1, False)
    asel(b("ident", 0, 128), b("zrep", 0, 128), [[-1, 128]], OP.is_equal, 0, 1)
    asel(b("bot", 0, 128), b("zrep", 0, 128), [[-16, 8], [0, 16]], OP.is_ge, 0, 1)
    asel(b("bo", 0, 128), b("bot", 0, 128), [[16, 8], [0, 16]], OP.is_ge, 15, -1)
    asel(b("lt", 0, 128), b("bo", 0, 128), [[1, 128]], OP.is_ge, -1, -1)
    ts(b("nident", 0, 128), b("ident", 0, 128), -1.0, OP.mult)
    send("i01")
    asel(b("rp", 0, 2048), b("zrep", 0, 2048), [[-1, 16], [-16, 8], [0, 16]], OP.is_equal, 0, 1)
    send("i2")
    send("i3")
    kl = b("kl", 0, 384)
    iota(kl, [[80, 3], [0, 8], [5, 16]], 17, 0)
    asel(kl, kl, [[0, 3], [-16, 8], [0, 16]], OP.is_ge, 0, 1)
    asel(kl, kl, [[0, 3], [16, 8], [0, 16]], OP.is_ge, 15, -1)
    asel(b("row0", 0, 128), b("one32", 0, 128), [[0, 128]], OP.is_equal, 0, 1)
    iota(b("i976", 0, 128), [[976, 128]], 0, 0)
    iota(b("gq", 0, 128), [[1, 8], [0, 16]], 0, 0)
    iota(b("vals", 0, 4096), [[1, 128], [0, 32]], 64, 0)
    asel(b("ind", 0, 2048), b("zrep", 0, 2048), [[-1, 128], [0, 16]], OP.is_equal, 0, 1)
    asel(b("dg", 0, 2048), b("rp", 0, 2048), [[-1, 16], [0, 8], [1, 16]], OP.is_equal, 0, 0)
    iota(b("zeros", 0, 8192), [[0, 8192]], 0, 0)

    ms(b("big", 0, 8192), 0.0)
    cp(b("bo32", 0, 128), b("bo", 0, 128))
    cp(b("lt32", 0, 128), b("lt", 0, 128))
    ts(b("woff", 8, 264), b("wt", 0, 256), 128.0, OP.add)

    def prefix_scan():
        scan(b("ex", 0, 257), b("m128", 0, 257), b("woff", 7, 264), OP.add, OP.add)

    def prefix_sums():
        mm(b("psM", 1, 2), b("lt32", 0, 128), b("ex", 256, 257), True, True)
        mm(b("psM", 2, 3), b("bo32", 0, 128), b("ex", 256, 257), True, True)

    def prefix_end():
        ts(b("off16", 0, 256), b("ex", 0, 256), b("psM", 1, 2), OP.add)

    prefix_scan()
    banks = (("psA", 0), ("psA", 512), ("psB", 0), ("psB", 512), ("psC0", 0), ("psC1", 0))
    for a in range(16):
        p = b(banks[a % 6][0], banks[a % 6][1], banks[a % 6][1] + 256)
        mm(p, b("ident", 0, 128), b("ptb", 16 + 256 * a, 272 + 256 * a), True, False)
        mm(p, b("nident", 0, 128), b("ptb", 15 + 256 * a, 271 + 256 * a), False, True)
        act(b("diffp", a, 4096, 16), p, AF.Copy, 0.0, 0.5)
    ms(b("mkx", 0, 2048), 512.0)
    ms(b("mkn", 0, 2048), -512.0)
    ms(b("mkx", 0, 2048, 16), -512.0)
    ms(b("mkn", 0, 2048, 16), 512.0)
    cp(b("lm16", 0, 1024), b("lmI", 0, 1024))
    cp(b("cb", 120, 128), b("bo", 0, 128, 16))
    ts(b("ncb", 0, 248), b("cb", 0, 248), -1.0, OP.mult)
    prefix_sums()
    prefix_end()
    ts(b("pI", 2, 3), b("pI", 0, 1), 7, OP.bitwise_and)
    cp(b("aF", 1, 2), b("pI", 2, 3))
    ts(b("pI", 1, 2), b("pI", 0, 1), 15, OP.bitwise_and)
    ts(b("aF", 2, 3), b("pI", 1, 2), 2.0, OP.mult, 1.0, OP.add)

    def inverse(c, k, n):
        m = 4096 // n
        w, v, off = b("invw", 0, 4096), b("vals", m * k, m * k + m), b("lm16", 256 * c + m // 16 * k, 256 * c + m // 16 * (k + 1))
        emit("s", lambda: g.scalar.activation(w[0].indirect(off[0]), v[0], AF.Silu), [v, off], [w])

    def inverse_table():
        dma("y", [((T.invt[a::16, 0:256], "invt", 0, 256), (T.invw[a::16, 256 * a:256 * a + 256], "invw", 0, 4096)) for a in range(16)])

    def inverse_list(c):
        ts(b("inv16", 256 * c, 256 * c + 256), b("invt", 0, 256), -63.75, OP.add)

    ZSRC = [(("zin0", 0), ("zin0", 128)), (("zr1", 0), ("zin1", 0)), (("zr2", 0), ("zin2", 0)), (("zr3", 0), ("zc0", 0))]
    MB, MO = ("ptb", "sg1"), (16, 0)
    MP = (("psA", 0), ("psA", 512), ("psC0", 0), ("psC1", 0))
    MXB = (("big", OMX), ("big", OMX + 2048), ("big", OMX + 4096))
    MNB = (("big", OMN), ("big", OMN + 2048), ("pE", 0))
    for t in range(ROUNDS):
        c0, c1 = t % 4, (t + 1) % 4
        last = t == ROUNDS - 1
        z0 = b(ZSRC[t][0][0], ZSRC[t][0][1], ZSRC[t][0][1] + 128)
        z1 = b(ZSRC[t][1][0], ZSRC[t][1][1], ZSRC[t][1][1] + 128)
        bigw, offs, dif = b("big", 0, 32768), b("off16", 0, 256), b("diffp", 0, 4096)
        emit("v", lambda: g.vector.tensor_copy(bigw[0].indirect(offs[0]), dif[0]), [dif, offs], [bigw])
        if t in WDMA:
            dma("y", [((T.wrep[a::16, :], "wrep", 0, 4096), b("woff", 8, 264)) for a in range(16)])
            inverse_table()
        else:
            for q in range(4):
                ps = ("psA", "psB")[q % 2]
                for k in range(4):
                    a = 4 * q + k
                    mm(b(ps, 256 * k, 256 * k + 256), b("rp", 128 * a, 128 * a + 128), b("woff", 8, 264), True, True)
                act(b("wrep", 1024 * q, 1024 * q + 1024), b(ps, 0, 1024), AF.Copy)
        if t == 0:
            act(kl, kl, AF.Copy, 0.0, b("aF", 2, 3))
        gath("s", b("ptb", 16, 4112), b("wrep", 0, 4096), b("lm16", 256 * c0, 256 * c0 + 256))
        if t == 0:
            inverse(0, 0, 1)
        act(b("wf", 0, 256), b("woff", 8, 264), AF.Copy, -128.0)
        act(b("zf32", 0, 128), z0, AF.Copy)
        mm(b("psC1", 0, 128), z0, b("ident", 0, 128), True, True)
        mm(b("psC1", 128, 256), z0, b("ident", 0, 128), True, False)
        mm(b("psC1", 128, 256), z1, b("nident", 0, 128), False, True)
        for k2 in range(3):
            p = b("psC0", 128 * k2, 128 * k2 + 128)
            mm(p, b("kl", 128 * k2, 128 * k2 + 128), b("zf32", 0, 128), True, False)
            mm(p, b("row0", 0, 128), b("i976", 0, 128), False, True)
        act(b("z0T", 0, 128), b("psC1", 0, 128), AF.Copy)
        act(b("dzT", 0, 128), b("psC1", 128, 256), AF.Copy)
        for q in range(4):
            mm(b(("psA", "psB")[q // 2], 512 * (q % 2), 512 * (q % 2) + 512), b("z0T", 0, 128), b("ind", 512 * q, 512 * q + 512), True, True)
        act(b("zrep", 0, 1024), b("psA", 0, 1024), AF.Copy)
        act(b("zrep", 1024, 2048), b("psB", 0, 1024), AF.Copy)
        for i in range(32):
            mm(b("psS", 0, 128), b("ident", 0, 128), b("ptb", 16 + i, 4112, 32), i == 0, i == 31)
        if t == 0:
            inverse_table()
            ts(b("orl", 0, 128), b("gq", 0, 128), b("aF", 1, 2), OP.is_equal)
        ts(b("smi", 0, 1), b("psM", 2, 3), 0.5, OP.mult, -0.25, OP.add)
        ts(b("thf", 0, 1), b("smi", 0, 1), 4096.0, OP.min, 1.0 / 2048.0, OP.mult)

        def heavy(r):
            ts(b("smv", 4, 5), b("acc", 1, 2), -16.0, OP.mult)
            ts(b("a16", 0, 1), b("acc", 0, 1), 16.0, OP.mult, b("smv", 4, 5), OP.add)
            ts(b("yab", r, r + 1), b("a16", 0, 1), 0.0625, OP.mult)

        if t > 0:
            heavy(t - 1)
        scan(b("pE", 0, 8192), b("big", 0, 8192), b("big", 0, 8192), OP.add, OP.add)
        if not last:
            dma("y", [(b("big", 0, 8192), b("zeros", 0, 8192))])
        else:
            dma("y", [(T.yz[:, 128:256], b("zf1", 0, 128)), (T.yz[:, 256:384], b("zf2", 0, 128))])
        if t == 0:
            gath("v", b("sg1", 0, 4096), b("wrep", 0, 4096), b("lm16", 256 * c1, 256 * c1 + 256))
        hI = b("hI", 0, 384)
        ts(hI, b("psC0", 0, 384), b("a16", 0, 1), OP.add)
        ts(hI, hI, 4, OP.arith_shift_right, 4095, OP.bitwise_and)
        ts(hI, hI, b("thf", 0, 1), OP.mult, -4095.5 + 1.0 / 4096.0, OP.add)
        ts(b("pos16", 0, 384), hI, 4095.0, OP.add)

        def two_sided(bk):
            return t == 0 and bk in VO

        def ring(m, bk, lo=0, step=1):
            base = (OA0, OA1)[m] + BLK * (bk % 4)
            return b("big", base + lo, base + BLK, step)

        def gather(bk):
            o, win, off = b("big", OD0 + bk * BLK, OD0 + bk * BLK + BLK), b("pE", 0, 8192), b("pos16", 64 * bk, 64 * bk + 64)
            zz = b("zrep", BLK * (bk % 2), BLK * (bk % 2) + BLK)
            emit("v", lambda: g.vector.tensor_tensor(o[0], win[0].indirect(off[0]), zz[0], OP.subtract), [win, off, zz], [o])
            if not two_sided(bk):
                act(ring(0, bk), o, AF.Abs)
            ps = ("psA", "psB")[bk % 2]
            for h in range(2):
                p = b(ps, 512 * h, 512 * h + 512)
                mm(p, b("ident", 0, 128), b("big", OD0 + bk * BLK + 512 * h, OD0 + bk * BLK + 512 * h + 512), True, False)
                mm(p, b("dzT", 0, 128), b("ind", BLK * (bk % 2) + 512 * h, BLK * (bk % 2) + 512 * h + 512), False, True)
            act(ring(1, bk), b(ps, 0, 1024), AF.Abs)
            if bk < 4:
                if t == 0:
                    inverse(1, bk, 4)
                else:
                    gath("s", b("sg1", BLK * bk, BLK * bk + BLK), b("wrep", 0, 4096), b("lm16", 256 * c1 + 64 * bk, 256 * c1 + 64 * bk + 64))

        def compare(bk):
            k2, half = bk // 2, bk % 2
            for m in range(2):
                two = m == 0 and two_sided(bk)
                o = b("psC%d" % m, 128 * k2 + 64 * half, 128 * k2 + 64 * half + 64)
                lo = BLK * half
                if two:
                    d = b("big", OD0 + bk * BLK, OD0 + bk * BLK + BLK)
                    ts(ring(0, bk), d, -68.0, OP.is_ge)
                    ts(b("b0r", lo, lo + BLK), d, 68.0, OP.is_gt)
                else:
                    ts(ring(m, bk), ring(m, bk), 68.0, OP.is_le)
                for a in range(16):
                    mm(o, b("cb", 120 - 8 * a, 248 - 8 * a), ring(m, bk, a, 16), a == 0, a == 15 and not two)
                if two:
                    for a in range(16):
                        mm(o, b("ncb", 120 - 8 * a, 248 - 8 * a), b("b0r", lo + a, lo + BLK, 16), False, a == 15)

        def extremes(k2, part=2):
            d = b("big", OD0 + 2048 * k2, OD0 + 2048 * k2 + 2048)
            if part != 1:
                scan(b(MXB[k2][0], MXB[k2][1], MXB[k2][1] + 2048), b("mkx", 0, 2048), d, OP.min, OP.max)
            if part != 0:
                scan(b(MNB[k2][0], MNB[k2][1], MNB[k2][1] + 2048), b("mkn", 0, 2048), d, OP.max, OP.min)

        def second_sums(h):
            for i in range(32):
                mm(b("psS", 128 + 64 * h, 192 + 64 * h), b("ident", 0, 128), b("sg1", 2048 * h + i, 2048 * h + 2048, 32), i == 0, i == 31)

        gather(0)
        gather(1)
        gather(2)
        if t == 0:
            inverse_list(0)
        compare(0)
        gather(3)
        compare(1)
        extremes(0)
        second_sums(0)
        gather(4)
        compare(2)
        gather(5)
        second_sums(1)
        extremes(1)
        compare(3)
        if t in (1, 2):
            inverse_list(t + 1)
        if t == 0:
            inverse_table()
        compare(4)
        extremes(2, 0)
        compare(5)
        ts(b("thr", 0, 256), b("psS", 0, 256), 4143.5, OP.is_lt, 0.5, OP.mult)
        extremes(2, 1)
        hits = (b("psM", 128, 256), b("psS", 256, 384))
        for m in range(2):
            act(b("hb%d" % m, 0, 384), b("psC%d" % m, 0, 384), AF.Relu, -11.0)
            for k2 in range(3):
                mm(hits[m], b("orl", 0, 128), b("hb%d" % m, 128 * k2, 128 * k2 + 128), k2 == 0, k2 == 2)
        tt(b("L01", 0, 128), hits[0], b("thr", 0, 128), OP.is_lt)
        ts(b("nh0", 0, 128), hits[0], 0.5, OP.is_ge)
        tt(b("x1", 0, 128), hits[1], b("thr", 128, 256), OP.is_lt)
        tt(b("L01", 128, 256), b("x1", 0, 128), b("nh0", 0, 128), OP.mult)

        def mark_gather(q, m, k0, k1):
            c = (c0, c1)[m]
            gath(q, b(MB[m], MO[m] + 512 * k0, MO[m] + 512 * k1), b("L01", 128 * m, 128 * m + 128),
                 b("inv16", 256 * c + 32 * k0, 256 * c + 32 * k1))

        def marks(m, h, first):
            p = b(MP[h][0], MP[h][1], MP[h][1] + 64)
            for a in range(16):
                mm(p, b("dg", 128 * a, 128 * a + 128), b(MB[m], MO[m] + 1024 * h + a, MO[m] + 1024 * h + 1024, 16),
                   first and a == 0, not first and a == 15)

        def extremes_end():
            for buf, o, op in ((MXB, "mx", OP.max), (MNB, "mn", OP.min)):
                e = [b(n, lo + 15, lo + 2048, 16) for n, lo in buf]
                tt(b(o, 0, 128), e[0], e[1], op)
                tt(b(o, 0, 128), b(o, 0, 128), e[2], op)
            ts(b("sel", 0, 128), hits[0], 0.5, OP.is_lt)
            ts(b("m1", 0, 128), hits[1], 0.5, OP.is_lt)
            tt(b("sel", 128, 256), b("m1", 0, 128), b("nh0", 0, 128), OP.mult)
            one, neg, mx, mn = b("ident", 0, 128), b("nident", 0, 128), b("mx", 0, 128), b("mn", 0, 128)
            for k, x in enumerate((mx, mn)):
                mm(b("psB", 0, 128), one, x, k == 0, k == 1)
            for k, (l, x) in enumerate(((one, mx), (one, mn), (one, z0), (one, z0), (neg, z1), (neg, z1))):
                mm(b("psB", 128, 256), l, x, k == 0, k == 5)

        def quarter():
            ts(b("q01", 0, 256), b("psB", 0, 256), 0.25, OP.mult, -0.375, OP.add)

        def move():
            tt(b("e01", 0, 256), b("q01", 0, 256), b("sel", 0, 256), OP.mult)
            for m, z in ((0, z0), (1, z1)):
                mm(b("psB", 512 + 128 * m, 640 + 128 * m), b("ident", 0, 128), b("e01", 128 * m, 128 * m + 128), True, False)
                mm(b("psB", 512 + 128 * m, 640 + 128 * m), b("ident", 0, 128), z, False, True)

        def hand_over():
            if t == 2:
                act(b("zo%d" % t, 0, 256), b("psB", 512, 768), AF.Copy)
            else:
                cp(b("zo%d" % t, 0, 256), b("psB", 512, 768))
            for kind in (("u0", "c0"), ("u1", "f1"), ("u2", "f2"), ("f3",))[t]:
                send(kind)

        if t == 0:
            ts(b("dg", 0, 2048), b("dg", 0, 2048), 8.0, OP.mult)
            inverse_list(1)
        mark_gather("s", 0, 0, 4)
        mark_gather("s", 0, 4, 8)
        if last:
            extremes_end()
            quarter()
            move()
            hand_over()
        marks(0, 0, True)
        marks(0, 1, True)
        mark_gather("v", 1, 0, 4)
        marks(1, 0, False)
        marks(1, 1, False)
        mark_gather("v", 1, 4, 6)
        marks(1, 2, True)
        marks(0, 2, False)
        marks(0, 3, True)
        mark_gather("s", 1, 6, 8)
        marks(1, 3, False)
        ts(b("w2", 0, 256), b("wf", 0, 256), 2.0, OP.mult, 8.0, OP.min)
        if not last:
            extremes_end()
        total(b("acc", 0, 1), b("sel", 0, 256))
        total(b("acc", 1, 2), b("L01", 0, 256))
        if t < 2:
            inverse(t + 2, 0, 1)
        for h in range(4):
            w1 = b("w1", 64 * h, 64 * h + 64)
            tt(w1, b(MP[h][0], MP[h][1], MP[h][1] + 64), b("w2", 64 * h, 64 * h + 64), OP.min)
            tt(w1, w1, b("wf", 64 * h, 64 * h + 64), OP.max)
        red(b("smv", 0, 1), b("w1", 0, 256))
        mm(b("psM", 0, 1), b("bo32", 0, 128), b("smv", 0, 1), True, True)
        if not last:
            quarter()
        ts(b("smv", 1, 2), b("psM", 0, 1), 7168.5, OP.is_gt, -0.5, OP.mult)
        ts(b("smv", 2, 3), b("smv", 1, 2), 1.0, OP.add)
        ts(b("smv", 3, 4), b("smv", 1, 2), -0.5, OP.mult, 128.0, OP.add)
        ts(b("woff", 8, 264), b("w1", 0, 256), b("smv", 2, 3), OP.mult, b("smv", 3, 4), OP.add)
        if not last:
            prefix_scan()
            prefix_sums()
            move()
            prefix_end()
            hand_over()

    ts(b("ywb", 0, 256), b("woff", 8, 264), -128.0, OP.add)
    dma("y", [(T.yw[:], b("ywb", 0, 256))])
    heavy(ROUNDS - 1)
    dma("y", [(T.ya[:], (T.yab[0::16, 0:4], "yab", 0, 4))])
    dma("s", [(T.yz[:, 384:512], b("zf3", 0, 128)), (T.yz[:, 0:128], b("zf3", 128, 256))])
    for sem, val in count.items():
        if waited["g"].get(sem, 0) < val:
            g.wait_ge(T.sem[sem], val)
